import numpy as np
import ml_dtypes


def mxq(x, axis, fmt="e4m3"):
    dtype, down = {"e4m3": (ml_dtypes.float8_e4m3fn, 7), "e5m2": (ml_dtypes.float8_e5m2, 14)}[fmt]
    v = np.moveaxis(np.asarray(x, np.float32).astype(ml_dtypes.bfloat16).astype(np.float64), axis, -1)
    blocks = v.reshape(v.shape[:-1] + (-1, 32))
    amax = np.abs(blocks).max(-1, keepdims=True)
    byte = np.maximum(np.where(amax > 0, np.frexp(amax)[1] - 1 + 127, 0) - down, 1)
    scale = np.exp2(byte - 127.0)
    codes = (blocks / scale).astype(np.float32).astype(dtype).astype(np.float64)
    return np.moveaxis((codes * scale).reshape(v.shape), -1, axis)


WIDE = False


def mx_kscale(k):
    if not WIDE:
        return np.ones(k)
    levels = np.array([10, -10, 5, -5, 0])
    if k % 512:
        return np.exp2(np.random.permutation(np.resize(levels, k // 32))).repeat(32)
    a = np.empty((k // 512, 16))
    for p in range(k // 512):
        a[p, :8] = np.random.permutation(np.resize(levels, 8))
        for g in range(8):
            far = levels[np.abs(levels - a[p, g]) >= 10]
            a[p, g + 8] = far[np.random.randint(len(far))]
    return np.exp2(a.ravel()).repeat(32)


def f64(x):
    return np.asarray(x).astype(np.float64)


def striped(idx):
    return np.tile(np.asarray(idx).reshape(-1, 16).T, (8, 1)).astype(np.uint16)


def unstriped(offs):
    return offs[:16].T.reshape(-1).astype(np.int64)


B, N, T, D, DV, NQ = 2, 512, 2048, 512, 512, 128


def setup_inputs():
    n = np.random.standard_normal
    seg = T // B
    idx = np.concatenate([b * seg + np.random.permutation(seg)[:N] for b in range(B)])
    s = mx_kscale(D)[:, None]
    u = np.ones(T)
    u[idx] = mx_kscale(B * N)
    r = np.random.uniform(0.5, 2.0, T)
    raw = n((D, T)) / s / (u * r)
    return {
        "qT": (n((B, D, NQ)) * s * (0.60 / np.sqrt(D))).astype(np.float32),
        "cT": raw.astype(np.float32),
        "ts": np.tile(u * r, (128, 1)).astype(np.float32),
        "ch": np.tile(s[:, 0] * np.random.uniform(0.5, 2.0, D), (128, 1)).astype(np.float32),
        "og": n((B, NQ, DV)).astype(np.float32),
        "offs": striped(idx),
    }


def reference(qT, cT, ts, ch, og, offs):
    idx = unstriped(offs)
    c = f64(cT)
    pick = lambda x: x[:, idx].reshape(x.shape[0], B, N).transpose(1, 0, 2)
    q = f64(qT)
    score = mxq(q, 1, "e4m3").transpose(0, 2, 1) @ mxq(pick(c), 1, "e4m3")
    score = score * pick(f64(ts))[:, :1, :]
    m = score.max(-1, keepdims=True)
    p = np.exp(score - m)
    total = p.sum(-1, keepdims=True)
    w = p * pick(f64(ts))[:, :1, :]
    y = mxq(w, 2, "e4m3") @ mxq(pick(c).transpose(0, 2, 1), 1, "e4m3")
    y = y / total
    y = y * f64(ch)[:1]
    y = y / (1.0 + np.exp(-f64(og)))
    return y

@@ -1,0 +1,306 @@
+from contextlib import ExitStack
+
+import concourse.mybir as mybir
+from concourse.masks import make_identity
+
+FLOPS = 2 * 2 * 2 * 128 * 512 * 512
+
+F32 = mybir.dt.float32
+BF16 = mybir.dt.bfloat16
+U32 = mybir.dt.uint32
+I32 = mybir.dt.int32
+U16 = mybir.dt.uint16
+U8 = mybir.dt.uint8
+FP8X4 = mybir.dt.float8_e4m3fn_x4
+MULT = mybir.AluOpType.mult
+ADD = mybir.AluOpType.add
+MAX = mybir.AluOpType.max
+COPY = mybir.ActivationFunctionType.Copy
+EXP = mybir.ActivationFunctionType.Exp
+TANH = mybir.ActivationFunctionType.Tanh
+AXIS_X = mybir.AxisListType.X
+
+P = 128
+B = 2
+N = 512
+T = 2048
+SEG = T // B
+D = 512
+NQ = 128
+HALF = SEG // 2
+LIST = N // 16
+ALL, LEFT, RIGHT = slice(0, N), slice(0, N // 2), slice(N // 2, N)
+
+
+def tile_attend_x_mla_gate_seg_kernel(tc, qT, cT, ts, ch, og, offs, out):
+    nc = tc.nc
+    with ExitStack() as ctx:
+        lists = ctx.enter_context(tc.tile_pool(name="lists", bufs=1))
+        keep = ctx.enter_context(tc.tile_pool(name="keep", bufs=1))
+        psum = ctx.enter_context(tc.psum_pool(name="psum", bufs=1))
+
+        offsets = lists.tile([P, B * LIST], U16, name="offsets")
+
+        def each(shape, dtype, name):
+            return [keep.tile(shape, dtype, name=f"{name}{b}", align_bytes=64) for b in range(B)]
+
+        raw = {(b, w, h): keep.tile([P, 2, HALF], F32, name=f"raw{b}{w}{h}") for b in range(B) for w in range(2) for h in range(2)}
+        scale_tab = keep.tile([P, T], F32, name="scale_tab")
+        q_raw = each([P, 4, NQ], F32, "q_raw")
+        ch_sb = keep.tile([P, D], F32, name="ch_sb")
+        og_sb = each([P, D], F32, "og_sb")
+        pairs = [keep.tile([P, T, 2], BF16, name=f"pairs{w}", align_bytes=64) for w in range(2)]
+        kb = each([P, N, 4], BF16, "kb")
+        k_codes, k_scales = each([P, N], U32, "k_codes"), each([P, N], U8, "k_scales")
+        q_bf = each([P, NQ, 4], BF16, "q_bf")
+        q_codes, q_scales = each([P, NQ], U32, "q_codes"), each([P, NQ], U8, "q_scales")
+        tsg = each([P, N], F32, "tsg")
+        ts_col = each([P, 4, 1], F32, "ts_col")
+        a = each([P, 4, P], F32, "a")
+        neg_m = each([P, 1], F32, "neg_m")
+        p = each([P, 4, P], F32, "p")
+        l_half = each([P, 2], F32, "l_half")
+        l_sum = each([P, 1], F32, "l_sum")
+        inv_l = each([P, 1], F32, "inv_l")
+        vb = each([P, D, 4], BF16, "vb")
+        v_codes, v_scales = each([P, D], U32, "v_codes"), each([P, D], U8, "v_scales")
+        wb = each([P, NQ, 4], BF16, "wb")
+        w_codes, w_scales = each([P, NQ], U32, "w_codes"), each([P, NQ], U8, "w_scales")
+        th = each([P, D], F32, "th")
+        gate = each([P, D], F32, "gate")
+        o = each([P, D], F32, "o")
+        bank = {}
+
+        ident = keep.tile([P, P], F32, name="ident")
+        make_identity(nc, ident[:])
+        warm = keep.tile([P, 1], F32, name="warm")
+        warmed = keep.tile([P, 1], F32, name="warmed")
+
+        def preload_exp():
+            nc.vector.memset(warm[:], 0.0)
+            nc.scalar.activation(out=warmed[:], in_=warm[:], func=EXP)
+
+        def load_pair(b, w, h):
+            n0 = b * SEG + h * HALF
+            nc.sync.dma_start(out=raw[b, w, h][:], in_=cT.rearrange("(p t) n -> p t n", t=4)[:, 2 * w : 2 * w + 2, n0 : n0 + HALF])
+
+        def load_scales(b):
+            nc.sync.dma_start(out=scale_tab[:, b * SEG : (b + 1) * SEG], in_=ts[:, b * SEG : (b + 1) * SEG])
+
+        def load_queries(b):
+            nc.sync.dma_start(out=q_raw[b][:], in_=qT[b].rearrange("(p t) q -> p t q", t=4))
+
+        def load_channels():
+            nc.sync.dma_start(out=ch_sb[:], in_=ch)
+
+        def load_gate(b):
+            nc.sync.dma_start(out=og_sb[b][:], in_=og[b])
+
+        def cast(engine, b, w, h):
+            n0 = b * SEG + h * HALF
+            dst = pairs[w][:, n0 : n0 + HALF, :]
+            src = raw[b, w, h][:].rearrange("p e n -> p n e")
+            if engine is nc.scalar:
+                nc.scalar.activation(out=dst, in_=src, func=COPY)
+            else:
+                nc.vector.tensor_copy(out=dst, in_=src)
+
+        def gather_pair(b, w):
+            window = pairs[w][:].rearrange("p n e -> p (n e)").bitcast(U32)
+            if b == 0:
+                window = window[:, 0:SEG]
+            dst = kb[b][:].rearrange("p n t -> p (n t)").bitcast(U32).rearrange("p (j s w) -> p w s j", j=4, w=2)[:, w]
+            nc.vector.tensor_copy(dst, window.indirect(offsets[:, b * LIST : (b + 1) * LIST]))
+
+        def gather_scales(b):
+            window = scale_tab[:].bitcast(U32)
+            if b == 0:
+                window = window[:, 0:SEG]
+            nc.vector.tensor_copy(tsg[b][:].bitcast(U32).rearrange("p (j s) -> p s j", j=4), window.indirect(offsets[:, b * LIST : (b + 1) * LIST]))
+
+        def turn_scales(b):
+            bank["ts", b] = psum.tile([P, 4, P], F32, name="scale_bank", tag="scale_bank")
+            for j in range(4):
+                nc.tensor.transpose(bank["ts", b][:, j, :], tsg[b][:, j * P : (j + 1) * P], ident[:])
+
+        def scale_column(b):
+            nc.scalar.activation(out=ts_col[b][:], in_=bank["ts", b][:, :, 0:1], func=COPY)
+
+        def cast_queries(b):
+            nc.gpsimd.tensor_scalar(q_bf[b][:], q_raw[b][:].rearrange("p t q -> p q t"), 1.0, 0.0, MULT, ADD)
+
+        def quantise(codes, scales, src):
+            nc.vector.quantize_mx(out=codes[:].bitcast(FP8X4), scales=scales[:], in_=src[:].rearrange("p n t -> p (n t)"))
+
+        def quantise_queries(b):
+            quantise(q_codes[b], q_scales[b], q_bf[b])
+
+        def quantise_keys(b, cols):
+            nc.vector.quantize_mx(
+                out=k_codes[b][:, cols].bitcast(FP8X4),
+                scales=k_scales[b][:, cols],
+                in_=kb[b][:, cols, :].rearrange("p n t -> p (n t)"),
+            )
+
+        def quantise_values(b):
+            quantise(v_codes[b], v_scales[b], vb[b])
+
+        def quantise_weights(b):
+            quantise(w_codes[b], w_scales[b], wb[b])
+
+        def scores(b, cols):
+            tile = psum.tile([P, cols.stop - cols.start], F32, name="result", tag="result", bufs=3)
+            bank["score", b, cols.start] = tile
+            nc.tensor.matmul_mx(
+                out=tile[:],
+                lhsT=q_codes[b][:].bitcast(FP8X4),
+                lhsT_scale=q_scales[b][:],
+                rhs=k_codes[b][:, cols].bitcast(FP8X4),
+                rhs_scale=k_scales[b][:, cols],
+                start=True,
+                stop=True,
+            )
+
+        def scale_scores(b, cols):
+            flat = a[b][:].rearrange("q j s -> q (j s)")
+            nc.vector.tensor_tensor(flat[:, cols], bank["score", b, cols.start][:], tsg[b][:, cols], MULT)
+
+        def maximum(b):
+            nc.vector.tensor_reduce(out=neg_m[b][:], in_=a[b][:].rearrange("q j s -> q (j s)"), axis=AXIS_X, op=MAX, negate=True)
+
+        def exponentials(b):
+            for h in range(2):
+                j2 = slice(2 * h, 2 * h + 2)
+                nc.scalar.activation(out=p[b][:, j2], in_=a[b][:, j2], func=EXP, bias=neg_m[b][:], accum_out=l_half[b][:, h : h + 1])
+
+        def invert_sums(b):
+            nc.gpsimd.tensor_scalar(l_sum[b][:], l_half[b][:, 0:1], l_half[b][:, 1:2], 2.0, ADD, MULT)
+            nc.vector.reciprocal(inv_l[b][:], l_sum[b][:])
+
+        def turn_values(b, w):
+            bank["v", b, w] = psum.tile([P, 4, P], F32, name="value_bank", tag="value_bank", bufs=3)
+            words = kb[b][:].rearrange("p n t -> p (n t)").bitcast(F32).rearrange("p (j s w) -> p w j s", j=4, w=2)
+            for j in range(4):
+                nc.tensor.transpose(bank["v", b, w][:, j, :], words[:, w, j, :], ident[:])
+
+        def copy_values(b, w):
+            src = bank["v", b, w][:].rearrange("s j p -> s (j p)").bitcast(BF16).rearrange("s (j p e) -> s p e j", j=4, e=2)
+            nc.scalar.activation(out=vb[b][:].rearrange("s (p w e) j -> s w p e j", w=2, e=2)[:, w], in_=src, func=COPY)
+
+        def turn_weights(b):
+            bank["w", b] = psum.tile([P, 4, P], F32, name="weight_bank", tag="weight_bank")
+            for j in range(4):
+                nc.tensor.transpose(bank["w", b][:, j, :], p[b][:, j, :], ident[:])
+
+        def scale_weights(b):
+            nc.vector.tensor_tensor(
+                wb[b][:],
+                bank["w", b][:].rearrange("s j q -> s q j"),
+                ts_col[b][:].rearrange("s j o -> s o j").to_broadcast([P, NQ, 4]),
+                MULT,
+            )
+
+        def products(b, cols):
+            tile = psum.tile([P, cols.stop - cols.start], F32, name="result", tag="result", bufs=3)
+            bank["y", b, cols.start] = tile
+            nc.tensor.matmul_mx(
+                out=tile[:],
+                lhsT=w_codes[b][:].bitcast(FP8X4),
+                lhsT_scale=w_scales[b][:],
+                rhs=v_codes[b][:, cols].bitcast(FP8X4),
+                rhs_scale=v_scales[b][:, cols],
+                start=True,
+                stop=True,
+            )
+
+        def gate_tanh(b):
+            nc.scalar.activation(out=th[b][:], in_=og_sb[b][:], func=TANH, scale=0.5)
+
+        def gate_channels(b):
+            nc.vector.scalar_tensor_tensor(out=gate[b][:], in0=th[b][:], scalar=1.0, in1=ch_sb[:], op0=ADD, op1=MULT)
+
+        def finish(b, cols):
+            y = bank["y", b, cols.start]
+            nc.vector.scalar_tensor_tensor(out=o[b][:, cols], in0=y[:], scalar=inv_l[b][:], in1=gate[b][:, cols], op0=MULT, op1=MULT)
+            nc.sync.dma_start(out=out[b][:, cols], in_=o[b][:, cols])
+
+        load_pair(0, 0, 0)
+        load_pair(0, 0, 1)
+        nc.sync.dma_start(offsets[:], offs)
+        load_pair(0, 1, 0)
+        load_pair(0, 1, 1)
+        load_queries(0)
+        load_pair(1, 0, 0)
+        load_pair(1, 0, 1)
+        load_scales(0)
+        load_pair(1, 1, 0)
+        load_pair(1, 1, 1)
+        load_queries(1)
+        load_scales(1)
+        load_channels()
+        load_gate(0)
+        load_gate(1)
+        preload_exp()
+        cast(nc.scalar, 0, 0, 0)
+        cast(nc.vector, 0, 0, 1)
+        cast(nc.scalar, 0, 1, 0)
+        gather_pair(0, 0)
+        cast_queries(0)
+        cast(nc.vector, 0, 1, 1)
+        turn_values(0, 0)
+        gather_pair(0, 1)
+        quantise_queries(0)
+        quantise_keys(0, ALL)
+        gather_scales(0)
+        cast(nc.scalar, 1, 0, 0)
+        scores(0, ALL)
+        turn_values(0, 1)
+        cast_queries(1)
+        turn_scales(0)
+        copy_values(0, 0)
+        cast(nc.scalar, 1, 0, 1)
+        scale_scores(0, ALL)
+        cast(nc.scalar, 1, 1, 0)
+        cast(nc.scalar, 1, 1, 1)
+        gather_pair(1, 0)
+        maximum(0)
+        turn_values(1, 0)
+        gather_pair(1, 1)
+        exponentials(0)
+        copy_values(0, 1)
+        quantise_queries(1)
+        quantise_keys(1, LEFT)
+        quantise_keys(1, RIGHT)
+        turn_weights(0)
+        gather_scales(1)
+        scores(1, LEFT)
+        scale_column(0)
+        scores(1, RIGHT)
+        invert_sums(0)
+        gate_tanh(0)
+        scale_scores(1, LEFT)
+        scale_scores(1, RIGHT)
+        scale_weights(0)
+        turn_values(1, 1)
+        copy_values(1, 0)
+        maximum(1)
+        turn_scales(1)
+        quantise_weights(0)
+        gate_tanh(1)
+        gate_channels(0)
+        quantise_values(0)
+        copy_values(1, 1)
+        quantise_values(1)
+        exponentials(1)
+        invert_sums(1)
+        scale_column(1)
+        turn_weights(1)
+        scale_weights(1)
+        products(0, ALL)
+        finish(0, ALL)
+        quantise_weights(1)
+        gate_channels(1)
+        products(1, LEFT)
+        products(1, RIGHT)
+        finish(1, LEFT)
+        finish(1, RIGHT)

@@ -42,9 +42,9 @@ def tile_attend_x_mla_gate_seg_kernel(tc, qT, cT, ts, ch, og, offs, out):
         offsets = lists.tile([P, B * LIST], U16, name="offsets")
 
         def each(shape, dtype, name):
-            return [keep.tile(shape, dtype, name=f"{name}{b}", align_bytes=64) for b in range(B)]
+            return [keep.tile(shape, dtype, name=f"{name}{b}", tag=f"{name}{b}", align_bytes=64) for b in range(B)]
 
-        raw = {(b, w, h): keep.tile([P, 2, HALF], F32, name=f"raw{b}{w}{h}") for b in range(B) for w in range(2) for h in range(2)}
+        raw = {(b, w, h): keep.tile([P, 2, HALF], F32, name=f"raw{b}{w}{h}", tag=f"raw{b}{w}{h}", align_bytes=64) for b in range(B) for w in range(2) for h in range(2)}
         scale_tab = keep.tile([P, T], F32, name="scale_tab")
         q_raw = each([P, 4, NQ], F32, "q_raw")
         ch_sb = keep.tile([P, D], F32, name="ch_sb")
@@ -55,24 +55,24 @@ def tile_attend_x_mla_gate_seg_kernel(tc, qT, cT, ts, ch, og, offs, out):
         q_bf = each([P, NQ, 4], BF16, "q_bf")
         q_codes, q_scales = each([P, NQ], U32, "q_codes"), each([P, NQ], U8, "q_scales")
         tsg = each([P, N], F32, "tsg")
-        ts_col = each([P, 4, 1], F32, "ts_col")
-        a = each([P, 4, P], F32, "a")
+        ts_col = {}
+        a_t = each([P, 4, NQ], F32, "a_t")
+        ts_rows = each([P, N], F32, "ts_rows")
         neg_m = each([P, 1], F32, "neg_m")
-        p = each([P, 4, P], F32, "p")
+        p = {1: keep.tile([P, 4, P], F32, name="p1")}
         l_half = each([P, 2], F32, "l_half")
-        l_sum = each([P, 1], F32, "l_sum")
-        inv_l = each([P, 1], F32, "inv_l")
-        vb = each([P, D, 4], BF16, "vb")
-        v_codes, v_scales = each([P, D], U32, "v_codes"), each([P, D], U8, "v_scales")
-        wb = each([P, NQ, 4], BF16, "wb")
+        l_sum = keep.tile([P, B], F32, name="l_sum")
+        inv_l = keep.tile([P, B], F32, name="inv_l")
+        vb = {}
+        v_codes, v_scales = {}, each([P, D], U8, "v_scales")
+        wb = {}
         w_codes, w_scales = each([P, NQ], U32, "w_codes"), each([P, NQ], U8, "w_scales")
         th = each([P, D], F32, "th")
-        gate = each([P, D], F32, "gate")
+        gate = {}
         o = each([P, D], F32, "o")
         bank = {}
 
         ident = keep.tile([P, P], F32, name="ident")
-        make_identity(nc, ident[:])
         warm = keep.tile([P, 1], F32, name="warm")
         warmed = keep.tile([P, 1], F32, name="warmed")
 
@@ -85,7 +85,9 @@ def tile_attend_x_mla_gate_seg_kernel(tc, qT, cT, ts, ch, og, offs, out):
             nc.sync.dma_start(out=raw[b, w, h][:], in_=cT.rearrange("(p t) n -> p t n", t=4)[:, 2 * w : 2 * w + 2, n0 : n0 + HALF])
 
         def load_scales(b):
-            nc.sync.dma_start(out=scale_tab[:, b * SEG : (b + 1) * SEG], in_=ts[:, b * SEG : (b + 1) * SEG])
+            cols = slice(b * SEG, (b + 1) * SEG)
+            (nc.gpsimd, nc.vector)[b].memset(scale_tab[:, cols], 0.0)
+            nc.sync.dma_start(out=scale_tab[0:1, cols], in_=ts[0:1, cols])
 
         def load_queries(b):
             nc.sync.dma_start(out=q_raw[b][:], in_=qT[b].rearrange("(p t) q -> p t q", t=4))
@@ -96,10 +98,10 @@ def tile_attend_x_mla_gate_seg_kernel(tc, qT, cT, ts, ch, og, offs, out):
         def load_gate(b):
             nc.sync.dma_start(out=og_sb[b][:], in_=og[b])
 
-        def cast(engine, b, w, h):
-            n0 = b * SEG + h * HALF
-            dst = pairs[w][:, n0 : n0 + HALF, :]
-            src = raw[b, w, h][:].rearrange("p e n -> p n e")
+        def cast(engine, b, w, h, c=0, width=HALF):
+            n0 = b * SEG + h * HALF + c
+            dst = pairs[w][:, n0 : n0 + width, :]
+            src = raw[b, w, h][:, :, c : c + width].rearrange("p e n -> p n e")
             if engine is nc.scalar:
                 nc.scalar.activation(out=dst, in_=src, func=COPY)
             else:
@@ -119,11 +121,12 @@ def tile_attend_x_mla_gate_seg_kernel(tc, qT, cT, ts, ch, og, offs, out):
             nc.vector.tensor_copy(tsg[b][:].bitcast(U32).rearrange("p (j s) -> p s j", j=4), window.indirect(offsets[:, b * LIST : (b + 1) * LIST]))
 
         def turn_scales(b):
-            bank["ts", b] = psum.tile([P, 4, P], F32, name="scale_bank", tag="scale_bank")
+            bank["ts", b] = psum.tile([P, 4, P], F32, name="bank", tag=f"bank{2 - b}")
             for j in range(4):
                 nc.tensor.transpose(bank["ts", b][:, j, :], tsg[b][:, j * P : (j + 1) * P], ident[:])
 
         def scale_column(b):
+            ts_col[b] = keep.tile([P, 4, 1], F32, name=f"ts_col{b}", tag=("raw001", "raw010")[b], align_bytes=64)
             nc.scalar.activation(out=ts_col[b][:], in_=bank["ts", b][:, :, 0:1], func=COPY)
 
         def cast_queries(b):
@@ -143,13 +146,22 @@ def tile_attend_x_mla_gate_seg_kernel(tc, qT, cT, ts, ch, og, offs, out):
             )
 
         def quantise_values(b):
+            v_codes[b] = keep.tile([P, D], U32, name="v_codes", tag=("ts_rows1", "v_codes1")[b], align_bytes=64)
             quantise(v_codes[b], v_scales[b], vb[b])
 
         def quantise_weights(b):
             quantise(w_codes[b], w_scales[b], wb[b])
 
-        def scores(b, cols):
-            tile = psum.tile([P, cols.stop - cols.start], F32, name="result", tag="result", bufs=3)
+        def spread_scales(b):
+            bank["tsb", b] = psum.tile([P, 4, P], F32, name="bank", tag=f"bank{3 + 2 * b}")
+            for j in range(4):
+                nc.tensor.transpose(bank["tsb", b][:, j, :], ts_col[b][:, j, :].to_broadcast([P, P]), ident[:])
+
+        def copy_spread(b):
+            nc.scalar.activation(out=ts_rows[b][:], in_=bank["tsb", b][:].rearrange("q j s -> q (j s)"), func=COPY)
+
+        def row_scores(b, cols):
+            tile = psum.tile([P, cols.stop - cols.start], F32, name="bank", tag=f"bank{6 + cols.start // 256 if b else 4}")
             bank["score", b, cols.start] = tile
             nc.tensor.matmul_mx(
                 out=tile[:],
@@ -161,24 +173,27 @@ def tile_attend_x_mla_gate_seg_kernel(tc, qT, cT, ts, ch, og, offs, out):
                 stop=True,
             )
 
-        def scale_scores(b, cols):
-            flat = a[b][:].rearrange("q j s -> q (j s)")
-            nc.vector.tensor_tensor(flat[:, cols], bank["score", b, cols.start][:], tsg[b][:, cols], MULT)
+        def scale_row_scores(b, cols):
+            flat = a_t[b][:].rearrange("q j s -> q (j s)")
+            nc.vector.tensor_tensor(flat[:, cols], bank["score", b, cols.start][:], ts_rows[b][:, cols], MULT)
+            bank["a", b] = a_t[b]
 
         def maximum(b):
-            nc.vector.tensor_reduce(out=neg_m[b][:], in_=a[b][:].rearrange("q j s -> q (j s)"), axis=AXIS_X, op=MAX, negate=True)
+            nc.vector.tensor_reduce(out=neg_m[b][:], in_=bank["a", b][:].rearrange("q j s -> q (j s)"), axis=AXIS_X, op=MAX, negate=True)
 
         def exponentials(b):
             for h in range(2):
                 j2 = slice(2 * h, 2 * h + 2)
-                nc.scalar.activation(out=p[b][:, j2], in_=a[b][:, j2], func=EXP, bias=neg_m[b][:], accum_out=l_half[b][:, h : h + 1])
+                nc.scalar.activation(out=p[b][:, j2], in_=bank["a", b][:, j2], func=EXP, bias=neg_m[b][:], accum_out=l_half[b][:, h : h + 1])
 
-        def invert_sums(b):
-            nc.gpsimd.tensor_scalar(l_sum[b][:], l_half[b][:, 0:1], l_half[b][:, 1:2], 2.0, ADD, MULT)
-            nc.vector.reciprocal(inv_l[b][:], l_sum[b][:])
+        def add_sums(b):
+            nc.gpsimd.tensor_scalar(l_sum[:, b : b + 1], l_half[b][:, 0:1], l_half[b][:, 1:2], 2.0, ADD, MULT)
+
+        def invert_sums():
+            nc.vector.reciprocal(inv_l[:], l_sum[:])
 
         def turn_values(b, w):
-            bank["v", b, w] = psum.tile([P, 4, P], F32, name="value_bank", tag="value_bank", bufs=3)
+            bank["v", b, w] = psum.tile([P, 4, P], F32, name="bank", tag=f"bank{(2 * b + w) % 3}")
             words = kb[b][:].rearrange("p n t -> p (n t)").bitcast(F32).rearrange("p (j s w) -> p w j s", j=4, w=2)
             for j in range(4):
                 nc.tensor.transpose(bank["v", b, w][:, j, :], words[:, w, j, :], ident[:])
@@ -188,11 +203,12 @@ def tile_attend_x_mla_gate_seg_kernel(tc, qT, cT, ts, ch, og, offs, out):
             nc.scalar.activation(out=vb[b][:].rearrange("s (p w e) j -> s w p e j", w=2, e=2)[:, w], in_=src, func=COPY)
 
         def turn_weights(b):
-            bank["w", b] = psum.tile([P, 4, P], F32, name="weight_bank", tag="weight_bank")
+            bank["w", b] = psum.tile([P, 4, P], F32, name="bank", tag=f"bank{3 + 2 * b}")
             for j in range(4):
                 nc.tensor.transpose(bank["w", b][:, j, :], p[b][:, j, :], ident[:])
 
         def scale_weights(b):
+            wb[b] = keep.tile([P, NQ, 4], BF16, name="wb", tag=("q_bf1", "wb1")[b], align_bytes=64)
             nc.vector.tensor_tensor(
                 wb[b][:],
                 bank["w", b][:].rearrange("s j q -> s q j"),
@@ -201,7 +217,7 @@ def tile_attend_x_mla_gate_seg_kernel(tc, qT, cT, ts, ch, og, offs, out):
             )
 
         def products(b, cols):
-            tile = psum.tile([P, cols.stop - cols.start], F32, name="result", tag="result", bufs=3)
+            tile = psum.tile([P, cols.stop - cols.start], F32, name="bank", tag=f"bank{6 + cols.start // 256 if b else 4}")
             bank["y", b, cols.start] = tile
             nc.tensor.matmul_mx(
                 out=tile[:],
@@ -213,94 +229,110 @@ def tile_attend_x_mla_gate_seg_kernel(tc, qT, cT, ts, ch, og, offs, out):
                 stop=True,
             )
 
+        def take_late():
+            late = keep.tile([P, 5 * N], F32, name="late", tag="raw111", align_bytes=64)
+            for b in range(B):
+                vb[b] = late[:, 2 * N * b : 2 * N * (b + 1)].bitcast(BF16).rearrange("s (c j) -> s c j", j=4)
+            p[0] = late[:, 4 * N : 5 * N].rearrange("q (j s) -> q j s", j=4)
+
         def gate_tanh(b):
             nc.scalar.activation(out=th[b][:], in_=og_sb[b][:], func=TANH, scale=0.5)
 
         def gate_channels(b):
+            if not gate:
+                both = keep.tile([P, B, D], F32, name="gate", tag="raw111", align_bytes=64)
+                gate[0], gate[1] = both[:, 0, :], both[:, 1, :]
             nc.vector.scalar_tensor_tensor(out=gate[b][:], in0=th[b][:], scalar=1.0, in1=ch_sb[:], op0=ADD, op1=MULT)
 
         def finish(b, cols):
             y = bank["y", b, cols.start]
-            nc.vector.scalar_tensor_tensor(out=o[b][:, cols], in0=y[:], scalar=inv_l[b][:], in1=gate[b][:, cols], op0=MULT, op1=MULT)
+            nc.vector.scalar_tensor_tensor(out=o[b][:, cols], in0=y[:], scalar=inv_l[:, b : b + 1], in1=gate[b][:, cols], op0=MULT, op1=MULT)
             nc.sync.dma_start(out=out[b][:, cols], in_=o[b][:, cols])
 
         load_pair(0, 0, 0)
-        load_pair(0, 0, 1)
+        load_scales(0)
         nc.sync.dma_start(offsets[:], offs)
+        load_scales(1)
+        load_pair(0, 0, 1)
         load_pair(0, 1, 0)
-        load_pair(0, 1, 1)
         load_queries(0)
+        load_pair(0, 1, 1)
         load_pair(1, 0, 0)
         load_pair(1, 0, 1)
-        load_scales(0)
         load_pair(1, 1, 0)
         load_pair(1, 1, 1)
         load_queries(1)
-        load_scales(1)
-        load_channels()
         load_gate(0)
+        load_channels()
         load_gate(1)
+        make_identity(nc, ident[:])
         preload_exp()
+        gather_scales(0)
+        gather_scales(1)
         cast(nc.scalar, 0, 0, 0)
-        cast(nc.vector, 0, 0, 1)
+        cast(nc.scalar, 0, 0, 1)
         cast(nc.scalar, 0, 1, 0)
+        turn_scales(0)
+        turn_scales(1)
         gather_pair(0, 0)
-        cast_queries(0)
+        scale_column(0)
+        scale_column(1)
         cast(nc.vector, 0, 1, 1)
+        spread_scales(0)
+        spread_scales(1)
         turn_values(0, 0)
+        copy_spread(0)
+        copy_spread(1)
+        cast_queries(0)
         gather_pair(0, 1)
+        cast(nc.scalar, 1, 0, 0)
         quantise_queries(0)
         quantise_keys(0, ALL)
-        gather_scales(0)
-        cast(nc.scalar, 1, 0, 0)
-        scores(0, ALL)
+        row_scores(0, ALL)
         turn_values(0, 1)
-        cast_queries(1)
-        turn_scales(0)
-        copy_values(0, 0)
-        cast(nc.scalar, 1, 0, 1)
-        scale_scores(0, ALL)
+        cast(nc.vector, 1, 0, 1)
+        scale_row_scores(0, ALL)
+        gather_pair(1, 0)
         cast(nc.scalar, 1, 1, 0)
         cast(nc.scalar, 1, 1, 1)
-        gather_pair(1, 0)
+        take_late()
         maximum(0)
-        turn_values(1, 0)
+        cast_queries(1)
         gather_pair(1, 1)
+        turn_values(1, 0)
+        copy_values(0, 0)
         exponentials(0)
-        copy_values(0, 1)
+        add_sums(0)
+        turn_weights(0)
         quantise_queries(1)
         quantise_keys(1, LEFT)
         quantise_keys(1, RIGHT)
-        turn_weights(0)
-        gather_scales(1)
-        scores(1, LEFT)
-        scale_column(0)
-        scores(1, RIGHT)
-        invert_sums(0)
-        gate_tanh(0)
-        scale_scores(1, LEFT)
-        scale_scores(1, RIGHT)
-        scale_weights(0)
+        row_scores(1, LEFT)
+        row_scores(1, RIGHT)
+        copy_values(0, 1)
         turn_values(1, 1)
-        copy_values(1, 0)
-        maximum(1)
-        turn_scales(1)
+        scale_weights(0)
+        scale_row_scores(1, LEFT)
+        scale_row_scores(1, RIGHT)
         quantise_weights(0)
-        gate_tanh(1)
-        gate_channels(0)
-        quantise_values(0)
+        maximum(1)
+        copy_values(1, 0)
         copy_values(1, 1)
-        quantise_values(1)
         exponentials(1)
-        invert_sums(1)
-        scale_column(1)
+        add_sums(1)
         turn_weights(1)
-        scale_weights(1)
+        gate_tanh(0)
+        gate_tanh(1)
+        quantise_values(0)
         products(0, ALL)
-        finish(0, ALL)
+        quantise_values(1)
+        gate_channels(0)
+        scale_weights(1)
+        invert_sums()
         quantise_weights(1)
-        gate_channels(1)
         products(1, LEFT)
         products(1, RIGHT)
+        finish(0, ALL)
+        gate_channels(1)
         finish(1, LEFT)
         finish(1, RIGHT)

@@ -49,16 +49,16 @@ def tile_attend_x_mla_gate_seg_kernel(tc, qT, cT, ts, ch, og, offs, out):
         q_raw = each([P, 4, NQ], F32, "q_raw")
         ch_sb = keep.tile([P, D], F32, name="ch_sb")
         og_sb = each([P, D], F32, "og_sb")
-        pairs = [keep.tile([P, T, 2], BF16, name=f"pairs{w}", align_bytes=64) for w in range(2)]
+        pairs = [keep.tile([P, T, 2], BF16, name=f"pairs{w}", tag=f"pairs{w}", align_bytes=64) for w in range(2)]
         kb = each([P, N, 4], BF16, "kb")
         k_codes, k_scales = each([P, N], U32, "k_codes"), each([P, N], U8, "k_scales")
         q_bf = each([P, NQ, 4], BF16, "q_bf")
         q_codes, q_scales = each([P, NQ], U32, "q_codes"), each([P, NQ], U8, "q_scales")
         tsg = each([P, N], F32, "tsg")
         ts_col = {}
-        a_t = each([P, 4, NQ], F32, "a_t")
-        ts_rows = each([P, N], F32, "ts_rows")
-        neg_m = each([P, 1], F32, "neg_m")
+        a_t = {1: keep.tile([P, 4, NQ], F32, name="a_t1")}
+        ts_rows = {}
+        neg_m = {}
         p = {1: keep.tile([P, 4, P], F32, name="p1")}
         l_half = each([P, 2], F32, "l_half")
         l_sum = keep.tile([P, B], F32, name="l_sum")
@@ -67,8 +67,8 @@ def tile_attend_x_mla_gate_seg_kernel(tc, qT, cT, ts, ch, og, offs, out):
         v_codes, v_scales = {}, each([P, D], U8, "v_scales")
         wb = {}
         w_codes, w_scales = each([P, NQ], U32, "w_codes"), each([P, NQ], U8, "w_scales")
-        th = each([P, D], F32, "th")
-        gate = {}
+        th = {}
+        gate = each([P, D], F32, "gate")
         o = each([P, D], F32, "o")
         bank = {}
 
@@ -86,7 +86,7 @@ def tile_attend_x_mla_gate_seg_kernel(tc, qT, cT, ts, ch, og, offs, out):
 
         def load_scales(b):
             cols = slice(b * SEG, (b + 1) * SEG)
-            (nc.gpsimd, nc.vector)[b].memset(scale_tab[:, cols], 0.0)
+            nc.vector.memset(scale_tab[:, cols], 0.0)
             nc.sync.dma_start(out=scale_tab[0:1, cols], in_=ts[0:1, cols])
 
         def load_queries(b):
@@ -126,7 +126,7 @@ def tile_attend_x_mla_gate_seg_kernel(tc, qT, cT, ts, ch, og, offs, out):
                 nc.tensor.transpose(bank["ts", b][:, j, :], tsg[b][:, j * P : (j + 1) * P], ident[:])
 
         def scale_column(b):
-            ts_col[b] = keep.tile([P, 4, 1], F32, name=f"ts_col{b}", tag=("raw001", "raw010")[b], align_bytes=64)
+            ts_col[b] = keep.tile([P, 4, 1], F32, name=f"ts_col{b}", tag=("raw010", "raw011")[b], align_bytes=64)
             nc.scalar.activation(out=ts_col[b][:], in_=bank["ts", b][:, :, 0:1], func=COPY)
 
         def cast_queries(b):
@@ -146,11 +146,34 @@ def tile_attend_x_mla_gate_seg_kernel(tc, qT, cT, ts, ch, og, offs, out):
             )
 
         def quantise_values(b):
-            v_codes[b] = keep.tile([P, D], U32, name="v_codes", tag=("ts_rows1", "v_codes1")[b], align_bytes=64)
+            v_codes[b] = keep.tile([P, D], U32, name="v_codes", tag=("v_codes0", "v_codes1")[b], align_bytes=64)
             quantise(v_codes[b], v_scales[b], vb[b])
 
         def quantise_weights(b):
             quantise(w_codes[b], w_scales[b], wb[b])
+
+        def scores(b):
+            bank["score", b] = psum.tile([P, 4, NQ], F32, name="bank", tag="bank4")
+            for j in range(4):
+                cols = slice(j * P, (j + 1) * P)
+                nc.tensor.matmul_mx(
+                    out=bank["score", b][:, j, :],
+                    lhsT=k_codes[b][:, cols].bitcast(FP8X4),
+                    lhsT_scale=k_scales[b][:, cols],
+                    rhs=q_codes[b][:].bitcast(FP8X4),
+                    rhs_scale=q_scales[b][:],
+                    start=True,
+                    stop=True,
+                )
+
+        def scale_scores(b):
+            a_t[b] = keep.tile([P, 4, NQ], F32, name="a_t0", tag="pairs0", align_bytes=64)
+            nc.vector.tensor_tensor(a_t[b][:], bank["score", b][:], ts_col[b][:].to_broadcast([P, 4, NQ]), MULT)
+
+        def turn_scores(b):
+            bank["a", b] = psum.tile([P, 4, P], F32, name="bank", tag="bank0")
+            for j in range(4):
+                nc.tensor.transpose(bank["a", b][:, j, :], a_t[b][:, j, :], ident[:])
 
         def spread_scales(b):
             bank["tsb", b] = psum.tile([P, 4, P], F32, name="bank", tag=f"bank{3 + 2 * b}")
@@ -179,6 +202,7 @@ def tile_attend_x_mla_gate_seg_kernel(tc, qT, cT, ts, ch, og, offs, out):
             bank["a", b] = a_t[b]
 
         def maximum(b):
+            neg_m[b] = keep.tile([P, 1], F32, name="neg_m", tag=("pairs1", "neg_m1")[b], align_bytes=64)
             nc.vector.tensor_reduce(out=neg_m[b][:], in_=bank["a", b][:].rearrange("q j s -> q (j s)"), axis=AXIS_X, op=MAX, negate=True)
 
         def exponentials(b):
@@ -193,7 +217,7 @@ def tile_attend_x_mla_gate_seg_kernel(tc, qT, cT, ts, ch, og, offs, out):
             nc.vector.reciprocal(inv_l[:], l_sum[:])
 
         def turn_values(b, w):
-            bank["v", b, w] = psum.tile([P, 4, P], F32, name="bank", tag=f"bank{(2 * b + w) % 3}")
+            bank["v", b, w] = psum.tile([P, 4, P], F32, name="bank", tag=f"bank{(3, 1, 2, 6)[2 * b + w]}")
             words = kb[b][:].rearrange("p n t -> p (n t)").bitcast(F32).rearrange("p (j s w) -> p w j s", j=4, w=2)
             for j in range(4):
                 nc.tensor.transpose(bank["v", b, w][:, j, :], words[:, w, j, :], ident[:])
@@ -203,12 +227,12 @@ def tile_attend_x_mla_gate_seg_kernel(tc, qT, cT, ts, ch, og, offs, out):
             nc.scalar.activation(out=vb[b][:].rearrange("s (p w e) j -> s w p e j", w=2, e=2)[:, w], in_=src, func=COPY)
 
         def turn_weights(b):
-            bank["w", b] = psum.tile([P, 4, P], F32, name="bank", tag=f"bank{3 + 2 * b}")
+            bank["w", b] = psum.tile([P, 4, P], F32, name="bank", tag=f"bank{4 + b}")
             for j in range(4):
                 nc.tensor.transpose(bank["w", b][:, j, :], p[b][:, j, :], ident[:])
 
         def scale_weights(b):
-            wb[b] = keep.tile([P, NQ, 4], BF16, name="wb", tag=("q_bf1", "wb1")[b], align_bytes=64)
+            wb[b] = keep.tile([P, NQ, 4], BF16, name="wb", tag=("wb0", "wb1")[b], align_bytes=64)
             nc.vector.tensor_tensor(
                 wb[b][:],
                 bank["w", b][:].rearrange("s j q -> s q j"),
@@ -217,7 +241,7 @@ def tile_attend_x_mla_gate_seg_kernel(tc, qT, cT, ts, ch, og, offs, out):
             )
 
         def products(b, cols):
-            tile = psum.tile([P, cols.stop - cols.start], F32, name="bank", tag=f"bank{6 + cols.start // 256 if b else 4}")
+            tile = psum.tile([P, cols.stop - cols.start], F32, name="bank", tag=f"bank{6 + cols.start // 256 if b else 0}")
             bank["y", b, cols.start] = tile
             nc.tensor.matmul_mx(
                 out=tile[:],
@@ -230,18 +254,17 @@ def tile_attend_x_mla_gate_seg_kernel(tc, qT, cT, ts, ch, og, offs, out):
             )
 
         def take_late():
-            late = keep.tile([P, 5 * N], F32, name="late", tag="raw111", align_bytes=64)
+            late = keep.tile([P, 8 * N], F32, name="late", tag="raw111", align_bytes=64)
             for b in range(B):
                 vb[b] = late[:, 2 * N * b : 2 * N * (b + 1)].bitcast(BF16).rearrange("s (c j) -> s c j", j=4)
+                th[b] = late[:, (5 + b) * N : (6 + b) * N]
+            ts_rows[1] = late[:, 7 * N : 8 * N]
             p[0] = late[:, 4 * N : 5 * N].rearrange("q (j s) -> q j s", j=4)
 
         def gate_tanh(b):
             nc.scalar.activation(out=th[b][:], in_=og_sb[b][:], func=TANH, scale=0.5)
 
         def gate_channels(b):
-            if not gate:
-                both = keep.tile([P, B, D], F32, name="gate", tag="raw111", align_bytes=64)
-                gate[0], gate[1] = both[:, 0, :], both[:, 1, :]
             nc.vector.scalar_tensor_tensor(out=gate[b][:], in0=th[b][:], scalar=1.0, in1=ch_sb[:], op0=ADD, op1=MULT)
 
         def finish(b, cols):
@@ -250,13 +273,13 @@ def tile_attend_x_mla_gate_seg_kernel(tc, qT, cT, ts, ch, og, offs, out):
             nc.sync.dma_start(out=out[b][:, cols], in_=o[b][:, cols])
 
         load_pair(0, 0, 0)
-        load_scales(0)
         nc.sync.dma_start(offsets[:], offs)
-        load_scales(1)
+        load_scales(0)
         load_pair(0, 0, 1)
+        load_scales(1)
         load_pair(0, 1, 0)
-        load_queries(0)
         load_pair(0, 1, 1)
+        load_queries(0)
         load_pair(1, 0, 0)
         load_pair(1, 0, 1)
         load_pair(1, 1, 0)
@@ -272,67 +295,66 @@ def tile_attend_x_mla_gate_seg_kernel(tc, qT, cT, ts, ch, og, offs, out):
         cast(nc.scalar, 0, 0, 0)
         cast(nc.scalar, 0, 0, 1)
         cast(nc.scalar, 0, 1, 0)
+        cast(nc.scalar, 0, 1, 1)
         turn_scales(0)
         turn_scales(1)
         gather_pair(0, 0)
         scale_column(0)
         scale_column(1)
-        cast(nc.vector, 0, 1, 1)
-        spread_scales(0)
         spread_scales(1)
         turn_values(0, 0)
-        copy_spread(0)
-        copy_spread(1)
         cast_queries(0)
+        quantise_queries(0)
         gather_pair(0, 1)
         cast(nc.scalar, 1, 0, 0)
-        quantise_queries(0)
+        cast(nc.scalar, 1, 0, 1)
         quantise_keys(0, ALL)
-        row_scores(0, ALL)
+        scores(0)
         turn_values(0, 1)
-        cast(nc.vector, 1, 0, 1)
-        scale_row_scores(0, ALL)
         gather_pair(1, 0)
         cast(nc.scalar, 1, 1, 0)
         cast(nc.scalar, 1, 1, 1)
         take_late()
-        maximum(0)
+        scale_scores(0)
         cast_queries(1)
         gather_pair(1, 1)
         turn_values(1, 0)
+        turn_scores(0)
+        copy_spread(1)
         copy_values(0, 0)
-        exponentials(0)
-        add_sums(0)
-        turn_weights(0)
+        copy_values(0, 1)
         quantise_queries(1)
         quantise_keys(1, LEFT)
         quantise_keys(1, RIGHT)
         row_scores(1, LEFT)
         row_scores(1, RIGHT)
-        copy_values(0, 1)
-        turn_values(1, 1)
-        scale_weights(0)
+        maximum(0)
+        copy_values(1, 0)
+        exponentials(0)
+        add_sums(0)
         scale_row_scores(1, LEFT)
         scale_row_scores(1, RIGHT)
-        quantise_weights(0)
+        turn_values(1, 1)
+        turn_weights(0)
+        quantise_values(0)
         maximum(1)
-        copy_values(1, 0)
-        copy_values(1, 1)
+        gate_tanh(0)
         exponentials(1)
         add_sums(1)
+        copy_values(1, 1)
+        scale_weights(0)
         turn_weights(1)
-        gate_tanh(0)
         gate_tanh(1)
-        quantise_values(0)
-        products(0, ALL)
-        quantise_values(1)
         gate_channels(0)
+        quantise_weights(0)
+        products(0, ALL)
         scale_weights(1)
         invert_sums()
+        quantise_values(1)
         quantise_weights(1)
         products(1, LEFT)
         products(1, RIGHT)
-        finish(0, ALL)
         gate_channels(1)
+        finish(0, ALL)
         finish(1, LEFT)
         finish(1, RIGHT)

@@ -47,7 +47,7 @@ def tile_attend_x_mla_gate_seg_kernel(tc, qT, cT, ts, ch, og, offs, out):
         raw = {(b, w, h): keep.tile([P, 2, HALF], F32, name=f"raw{b}{w}{h}", tag=f"raw{b}{w}{h}", align_bytes=64) for b in range(B) for w in range(2) for h in range(2)}
         scale_tab = keep.tile([P, T], F32, name="scale_tab")
         q_raw = each([P, 4, NQ], F32, "q_raw")
-        ch_sb = keep.tile([P, D], F32, name="ch_sb")
+        ch_col = keep.tile([P, 4], F32, name="ch_col")
         og_sb = each([P, D], F32, "og_sb")
         pairs = [keep.tile([P, T, 2], BF16, name=f"pairs{w}", tag=f"pairs{w}", align_bytes=64) for w in range(2)]
         kb = each([P, N, 4], BF16, "kb")
@@ -93,7 +93,12 @@ def tile_attend_x_mla_gate_seg_kernel(tc, qT, cT, ts, ch, og, offs, out):
             nc.sync.dma_start(out=q_raw[b][:], in_=qT[b].rearrange("(p t) q -> p t q", t=4))
 
         def load_channels():
-            nc.sync.dma_start(out=ch_sb[:], in_=ch)
+            nc.sync.dma_start(out=ch_col[:], in_=ch[0].rearrange("(p t) -> p t", t=4))
+
+        def spread_channels():
+            bank["ch"] = psum.tile([P, 4, P], F32, name="bank", tag="bank3")
+            for t in range(4):
+                nc.tensor.transpose(bank["ch"][:, t, :], ch_col[:, t : t + 1].to_broadcast([P, P]), ident[:])
 
         def load_gate(b):
             nc.sync.dma_start(out=og_sb[b][:], in_=og[b])
@@ -265,7 +270,14 @@ def tile_attend_x_mla_gate_seg_kernel(tc, qT, cT, ts, ch, og, offs, out):
             nc.scalar.activation(out=th[b][:], in_=og_sb[b][:], func=TANH, scale=0.5)
 
         def gate_channels(b):
-            nc.vector.scalar_tensor_tensor(out=gate[b][:], in0=th[b][:], scalar=1.0, in1=ch_sb[:], op0=ADD, op1=MULT)
+            nc.vector.scalar_tensor_tensor(
+                out=gate[b][:].rearrange("q (p t) -> q p t", t=4),
+                in0=th[b][:].rearrange("q (p t) -> q p t", t=4),
+                scalar=1.0,
+                in1=bank["ch"][:].rearrange("q t p -> q p t"),
+                op0=ADD,
+                op1=MULT,
+            )
 
         def finish(b, cols):
             y = bank["y", b, cols.start]
@@ -288,7 +300,8 @@ def tile_attend_x_mla_gate_seg_kernel(tc, qT, cT, ts, ch, og, offs, out):
         load_gate(0)
         load_channels()
         load_gate(1)
-        make_identity(nc, ident[:])
+        nc.vector.memset(ident[:], 0.0)
+        make_identity(nc, ident[:], nomemset=True)
         preload_exp()
         gather_scales(0)
         gather_scales(1)
@@ -322,6 +335,7 @@ def tile_attend_x_mla_gate_seg_kernel(tc, qT, cT, ts, ch, og, offs, out):
         turn_scores(0)
         copy_spread(1)
         copy_values(0, 0)
+        spread_channels()
         copy_values(0, 1)
         quantise_queries(1)
         quantise_keys(1, LEFT)

@@ -58,7 +58,7 @@ def tile_attend_x_mla_gate_seg_kernel(tc, qT, cT, ts, ch, og, offs, out):
         ts_col = {}
         a_t = {1: keep.tile([P, 4, NQ], F32, name="a_t1")}
         ts_rows = {}
-        neg_m = {}
+        neg_m = {1: keep.tile([P, 1], F32, name="neg_m1")}
         p = {1: keep.tile([P, 4, P], F32, name="p1")}
         l_half = each([P, 2], F32, "l_half")
         l_sum = keep.tile([P, B], F32, name="l_sum")
@@ -86,7 +86,7 @@ def tile_attend_x_mla_gate_seg_kernel(tc, qT, cT, ts, ch, og, offs, out):
 
         def load_scales(b):
             cols = slice(b * SEG, (b + 1) * SEG)
-            nc.vector.memset(scale_tab[:, cols], 0.0)
+            nc.vector.memset(scale_tab[:, cols].bitcast(I32), 0)
             nc.sync.dma_start(out=scale_tab[0:1, cols], in_=ts[0:1, cols])
 
         def load_queries(b):
@@ -105,8 +105,8 @@ def tile_attend_x_mla_gate_seg_kernel(tc, qT, cT, ts, ch, og, offs, out):
 
         def cast(engine, b, w, h, c=0, width=HALF):
             n0 = b * SEG + h * HALF + c
-            dst = pairs[w][:, n0 : n0 + width, :]
-            src = raw[b, w, h][:, :, c : c + width].rearrange("p e n -> p n e")
+            dst = pairs[w][:, n0 : n0 + width, :].rearrange("p (n i) e -> p n e i", i=4)
+            src = raw[b, w, h][:, :, c : c + width].rearrange("p e (n i) -> p n e i", i=4)
             if engine is nc.scalar:
                 nc.scalar.activation(out=dst, in_=src, func=COPY)
             else:
@@ -172,7 +172,7 @@ def tile_attend_x_mla_gate_seg_kernel(tc, qT, cT, ts, ch, og, offs, out):
                 )
 
         def scale_scores(b):
-            a_t[b] = keep.tile([P, 4, NQ], F32, name="a_t0", tag="pairs0", align_bytes=64)
+            a_t[b] = keep.tile([P, 4, NQ], F32, name="a_t0", tag="raw101", align_bytes=64)
             nc.vector.tensor_tensor(a_t[b][:], bank["score", b][:], ts_col[b][:].to_broadcast([P, 4, NQ]), MULT)
 
         def turn_scores(b):
@@ -207,7 +207,6 @@ def tile_attend_x_mla_gate_seg_kernel(tc, qT, cT, ts, ch, og, offs, out):
             bank["a", b] = a_t[b]
 
         def maximum(b):
-            neg_m[b] = keep.tile([P, 1], F32, name="neg_m", tag=("pairs1", "neg_m1")[b], align_bytes=64)
             nc.vector.tensor_reduce(out=neg_m[b][:], in_=bank["a", b][:].rearrange("q j s -> q (j s)"), axis=AXIS_X, op=MAX, negate=True)
 
         def exponentials(b):
@@ -228,8 +227,8 @@ def tile_attend_x_mla_gate_seg_kernel(tc, qT, cT, ts, ch, og, offs, out):
                 nc.tensor.transpose(bank["v", b, w][:, j, :], words[:, w, j, :], ident[:])
 
         def copy_values(b, w):
-            src = bank["v", b, w][:].rearrange("s j p -> s (j p)").bitcast(BF16).rearrange("s (j p e) -> s p e j", j=4, e=2)
-            nc.scalar.activation(out=vb[b][:].rearrange("s (p w e) j -> s w p e j", w=2, e=2)[:, w], in_=src, func=COPY)
+            src = bank["v", b, w][:].rearrange("s j p -> s (j p)").bitcast(BF16).rearrange("s (j p e) -> s p j e", j=4, e=2)
+            nc.scalar.activation(out=vb[b][:].rearrange("s (p w e) j -> s w p j e", w=2, e=2)[:, w], in_=src, func=COPY)
 
         def turn_weights(b):
             bank["w", b] = psum.tile([P, 4, P], F32, name="bank", tag=f"bank{4 + b}")
@@ -239,9 +238,9 @@ def tile_attend_x_mla_gate_seg_kernel(tc, qT, cT, ts, ch, og, offs, out):
         def scale_weights(b):
             wb[b] = keep.tile([P, NQ, 4], BF16, name="wb", tag=("wb0", "wb1")[b], align_bytes=64)
             nc.vector.tensor_tensor(
-                wb[b][:],
-                bank["w", b][:].rearrange("s j q -> s q j"),
-                ts_col[b][:].rearrange("s j o -> s o j").to_broadcast([P, NQ, 4]),
+                wb[b][:].rearrange("s (q i) j -> s q j i", i=2),
+                bank["w", b][:].rearrange("s j (q i) -> s q j i", i=2),
+                ts_col[b][:].unsqueeze(1).to_broadcast([P, NQ // 2, 4, 2]),
                 MULT,
             )
 
@@ -259,11 +258,12 @@ def tile_attend_x_mla_gate_seg_kernel(tc, qT, cT, ts, ch, og, offs, out):
             )
 
         def take_late():
-            late = keep.tile([P, 8 * N], F32, name="late", tag="raw111", align_bytes=64)
+            late = keep.tile([P, 8 * N + 8], F32, name="late", tag="raw111", align_bytes=64)
             for b in range(B):
                 vb[b] = late[:, 2 * N * b : 2 * N * (b + 1)].bitcast(BF16).rearrange("s (c j) -> s c j", j=4)
                 th[b] = late[:, (5 + b) * N : (6 + b) * N]
             ts_rows[1] = late[:, 7 * N : 8 * N]
+            neg_m[0] = late[:, 8 * N : 8 * N + 1]
             p[0] = late[:, 4 * N : 5 * N].rearrange("q (j s) -> q j s", j=4)
 
         def gate_tanh(b):

@@ -27,9 +27,9 @@ T = 2048
 SEG = T // B
 D = 512
 NQ = 128
-HALF = SEG // 2
 LIST = N // 16
 ALL, LEFT, RIGHT = slice(0, N), slice(0, N // 2), slice(N // 2, N)
+EVERY, LOW, HIGH = slice(0, 4), slice(0, 2), slice(2, 4)
 
 
 def tile_attend_x_mla_gate_seg_kernel(tc, qT, cT, ts, ch, og, offs, out):
@@ -41,48 +41,49 @@ def tile_attend_x_mla_gate_seg_kernel(tc, qT, cT, ts, ch, og, offs, out):
 
         offsets = lists.tile([P, B * LIST], U16, name="offsets")
 
-        def each(shape, dtype, name):
-            return [keep.tile(shape, dtype, name=f"{name}{b}", tag=f"{name}{b}", align_bytes=64) for b in range(B)]
+        def new(shape, dtype, name, tag=None):
+            return keep.tile(shape, dtype, name=name, tag=tag or name, align_bytes=64)
 
-        raw = {(b, w, h): keep.tile([P, 2, HALF], F32, name=f"raw{b}{w}{h}", tag=f"raw{b}{w}{h}", align_bytes=64) for b in range(B) for w in range(2) for h in range(2)}
-        scale_tab = keep.tile([P, T], F32, name="scale_tab")
+        def each(shape, dtype, name):
+            return [new(shape, dtype, f"{name}{b}") for b in range(B)]
+
+        win = {(b, t): new([P, (b + 1) * SEG], F32, f"win{b}{t}") for b in range(B) for t in range(4)}
+        scale_tab = new([P, T], F32, "scale_tab")
         q_raw = each([P, 4, NQ], F32, "q_raw")
-        ch_col = keep.tile([P, 4], F32, name="ch_col")
+        ch_col = new([P, 4], F32, "ch_col")
         og_sb = each([P, D], F32, "og_sb")
-        pairs = [keep.tile([P, T, 2], BF16, name=f"pairs{w}", tag=f"pairs{w}", align_bytes=64) for w in range(2)]
-        kb = each([P, N, 4], BF16, "kb")
+        planes = each([P, 4 * N], BF16, "planes")
+        kb = each([P, 4 * N], BF16, "kb")
         k_codes, k_scales = each([P, N], U32, "k_codes"), each([P, N], U8, "k_scales")
         q_bf = each([P, NQ, 4], BF16, "q_bf")
         q_codes, q_scales = each([P, NQ], U32, "q_codes"), each([P, NQ], U8, "q_scales")
         tsg = each([P, N], F32, "tsg")
-        ts_col = {}
-        a_t = {1: keep.tile([P, 4, NQ], F32, name="a_t1")}
-        ts_rows = {}
-        neg_m = {1: keep.tile([P, 1], F32, name="neg_m1")}
-        p = {1: keep.tile([P, 4, P], F32, name="p1")}
+        ts_col, neg_m, p, vb = {}, {}, {}, {}
+        a_t = each([P, 4, P], F32, "a_t")
+        neg_m[1] = new([P, 1], F32, "neg_m1")
+        p[1] = new([P, 4, P], F32, "p1")
         l_half = each([P, 2], F32, "l_half")
-        l_sum = keep.tile([P, B], F32, name="l_sum")
-        inv_l = keep.tile([P, B], F32, name="inv_l")
-        vb = {}
-        v_codes, v_scales = {}, each([P, D], U8, "v_scales")
-        wb = {}
+        l_sum = each([P, 1], F32, "l_sum")
+        inv_l = each([P, 1], F32, "inv_l")
+        v_codes, v_scales = {1: new([P, D], U32, "v_codes1")}, each([P, D], U8, "v_scales")
+        wb = each([P, NQ, 4], BF16, "wb")
         w_codes, w_scales = each([P, NQ], U32, "w_codes"), each([P, NQ], U8, "w_scales")
-        th = {}
-        gate = each([P, D], F32, "gate")
+        th = each([P, D], F32, "th")
+        gate = {1: new([P, D], F32, "gate1")}
         o = each([P, D], F32, "o")
         bank = {}
 
-        ident = keep.tile([P, P], F32, name="ident")
-        warm = keep.tile([P, 1], F32, name="warm")
-        warmed = keep.tile([P, 1], F32, name="warmed")
+        ident = new([P, P], F32, "ident")
+        warm = new([P, 1], F32, "warm")
+        warmed = new([P, 1], F32, "warmed")
 
         def preload_exp():
             nc.vector.memset(warm[:], 0.0)
             nc.scalar.activation(out=warmed[:], in_=warm[:], func=EXP)
 
-        def load_pair(b, w, h):
-            n0 = b * SEG + h * HALF
-            nc.sync.dma_start(out=raw[b, w, h][:], in_=cT.rearrange("(p t) n -> p t n", t=4)[:, 2 * w : 2 * w + 2, n0 : n0 + HALF])
+        def load_plane(b, t):
+            cols = slice(b * SEG, (b + 1) * SEG)
+            nc.sync.dma_start(out=win[b, t][:, cols], in_=cT.rearrange("(p t) n -> p t n", t=4)[:, t, cols])
 
         def load_scales(b):
             cols = slice(b * SEG, (b + 1) * SEG)
@@ -103,21 +104,21 @@ def tile_attend_x_mla_gate_seg_kernel(tc, qT, cT, ts, ch, og, offs, out):
         def load_gate(b):
             nc.sync.dma_start(out=og_sb[b][:], in_=og[b])
 
-        def cast(engine, b, w, h, c=0, width=HALF):
-            n0 = b * SEG + h * HALF + c
-            dst = pairs[w][:, n0 : n0 + width, :].rearrange("p (n i) e -> p n e i", i=4)
-            src = raw[b, w, h][:, :, c : c + width].rearrange("p e (n i) -> p n e i", i=4)
+        def gather_plane(engine, b, t, cols=ALL):
+            dst = planes[b][:, t * N + cols.start : t * N + cols.stop]
+            src = win[b, t][:].indirect(offsets[:, b * LIST + cols.start // 16 : b * LIST + cols.stop // 16])
             if engine is nc.scalar:
                 nc.scalar.activation(out=dst, in_=src, func=COPY)
             else:
                 nc.vector.tensor_copy(out=dst, in_=src)
 
-        def gather_pair(b, w):
-            window = pairs[w][:].rearrange("p n e -> p (n e)").bitcast(U32)
-            if b == 0:
-                window = window[:, 0:SEG]
-            dst = kb[b][:].rearrange("p n t -> p (n t)").bitcast(U32).rearrange("p (j s w) -> p w s j", j=4, w=2)[:, w]
-            nc.vector.tensor_copy(dst, window.indirect(offsets[:, b * LIST : (b + 1) * LIST]))
+        def weave(engine, b, js):
+            dst = kb[b][:].rearrange("p (j c i t) -> p c t i j", j=4, i=2, t=4)[:, :, :, :, js]
+            src = planes[b][:].rearrange("p (t c i j) -> p c t i j", t=4, i=2, j=4)[:, :, :, :, js]
+            if engine is nc.scalar:
+                nc.scalar.copy(out=dst, in_=src)
+            else:
+                nc.vector.tensor_copy(out=dst, in_=src)
 
         def gather_scales(b):
             window = scale_tab[:].bitcast(U32)
@@ -131,38 +132,33 @@ def tile_attend_x_mla_gate_seg_kernel(tc, qT, cT, ts, ch, og, offs, out):
                 nc.tensor.transpose(bank["ts", b][:, j, :], tsg[b][:, j * P : (j + 1) * P], ident[:])
 
         def scale_column(b):
-            ts_col[b] = keep.tile([P, 4, 1], F32, name=f"ts_col{b}", tag=("raw010", "raw011")[b], align_bytes=64)
             nc.scalar.activation(out=ts_col[b][:], in_=bank["ts", b][:, :, 0:1], func=COPY)
 
         def cast_queries(b):
             nc.gpsimd.tensor_scalar(q_bf[b][:], q_raw[b][:].rearrange("p t q -> p q t"), 1.0, 0.0, MULT, ADD)
 
         def quantise(codes, scales, src):
-            nc.vector.quantize_mx(out=codes[:].bitcast(FP8X4), scales=scales[:], in_=src[:].rearrange("p n t -> p (n t)"))
+            nc.vector.quantize_mx(out=codes.bitcast(FP8X4), scales=scales, in_=src)
 
         def quantise_queries(b):
-            quantise(q_codes[b], q_scales[b], q_bf[b])
+            quantise(q_codes[b][:], q_scales[b][:], q_bf[b][:].rearrange("p n t -> p (n t)"))
 
         def quantise_keys(b, cols):
-            nc.vector.quantize_mx(
-                out=k_codes[b][:, cols].bitcast(FP8X4),
-                scales=k_scales[b][:, cols],
-                in_=kb[b][:, cols, :].rearrange("p n t -> p (n t)"),
-            )
+            quantise(k_codes[b][:, cols], k_scales[b][:, cols], kb[b][:, 4 * cols.start : 4 * cols.stop])
 
         def quantise_values(b):
-            v_codes[b] = keep.tile([P, D], U32, name="v_codes", tag=("v_codes0", "v_codes1")[b], align_bytes=64)
-            quantise(v_codes[b], v_scales[b], vb[b])
+            quantise(v_codes[b][:], v_scales[b][:], vb[b][:])
 
         def quantise_weights(b):
-            quantise(w_codes[b], w_scales[b], wb[b])
+            quantise(w_codes[b][:], w_scales[b][:], wb[b][:].rearrange("p n t -> p (n t)"))
 
-        def scores(b):
-            bank["score", b] = psum.tile([P, 4, NQ], F32, name="bank", tag="bank4")
-            for j in range(4):
+        def scores(b, js, tag):
+            tile = psum.tile([P, js.stop - js.start, NQ], F32, name="bank", tag=tag)
+            for j in range(js.start, js.stop):
+                bank["score", b, j] = tile[:, j - js.start, :]
                 cols = slice(j * P, (j + 1) * P)
                 nc.tensor.matmul_mx(
-                    out=bank["score", b][:, j, :],
+                    out=bank["score", b, j],
                     lhsT=k_codes[b][:, cols].bitcast(FP8X4),
                     lhsT_scale=k_scales[b][:, cols],
                     rhs=q_codes[b][:].bitcast(FP8X4),
@@ -170,41 +166,19 @@ def tile_attend_x_mla_gate_seg_kernel(tc, qT, cT, ts, ch, og, offs, out):
                     start=True,
                     stop=True,
                 )
+            bank["score", b] = tile
 
         def scale_scores(b):
-            a_t[b] = keep.tile([P, 4, NQ], F32, name="a_t0", tag="raw101", align_bytes=64)
             nc.vector.tensor_tensor(a_t[b][:], bank["score", b][:], ts_col[b][:].to_broadcast([P, 4, NQ]), MULT)
 
-        def turn_scores(b):
-            bank["a", b] = psum.tile([P, 4, P], F32, name="bank", tag="bank0")
-            for j in range(4):
+        def scale_block(b, j):
+            nc.scalar.activation(out=a_t[b][:, j, :], in_=bank["score", b, j], func=COPY, scale=ts_col[b][:, j, :])
+
+        def turn_scores(b, js):
+            if js.start == 0:
+                bank["a", b] = psum.tile([P, 4, P], F32, name="bank", tag=("bank0", "bank5")[b])
+            for j in range(js.start, js.stop):
                 nc.tensor.transpose(bank["a", b][:, j, :], a_t[b][:, j, :], ident[:])
-
-        def spread_scales(b):
-            bank["tsb", b] = psum.tile([P, 4, P], F32, name="bank", tag=f"bank{3 + 2 * b}")
-            for j in range(4):
-                nc.tensor.transpose(bank["tsb", b][:, j, :], ts_col[b][:, j, :].to_broadcast([P, P]), ident[:])
-
-        def copy_spread(b):
-            nc.scalar.activation(out=ts_rows[b][:], in_=bank["tsb", b][:].rearrange("q j s -> q (j s)"), func=COPY)
-
-        def row_scores(b, cols):
-            tile = psum.tile([P, cols.stop - cols.start], F32, name="bank", tag=f"bank{6 + cols.start // 256 if b else 4}")
-            bank["score", b, cols.start] = tile
-            nc.tensor.matmul_mx(
-                out=tile[:],
-                lhsT=q_codes[b][:].bitcast(FP8X4),
-                lhsT_scale=q_scales[b][:],
-                rhs=k_codes[b][:, cols].bitcast(FP8X4),
-                rhs_scale=k_scales[b][:, cols],
-                start=True,
-                stop=True,
-            )
-
-        def scale_row_scores(b, cols):
-            flat = a_t[b][:].rearrange("q j s -> q (j s)")
-            nc.vector.tensor_tensor(flat[:, cols], bank["score", b, cols.start][:], ts_rows[b][:, cols], MULT)
-            bank["a", b] = a_t[b]
 
         def maximum(b):
             nc.vector.tensor_reduce(out=neg_m[b][:], in_=bank["a", b][:].rearrange("q j s -> q (j s)"), axis=AXIS_X, op=MAX, negate=True)
@@ -215,28 +189,29 @@ def tile_attend_x_mla_gate_seg_kernel(tc, qT, cT, ts, ch, og, offs, out):
                 nc.scalar.activation(out=p[b][:, j2], in_=bank["a", b][:, j2], func=EXP, bias=neg_m[b][:], accum_out=l_half[b][:, h : h + 1])
 
         def add_sums(b):
-            nc.gpsimd.tensor_scalar(l_sum[:, b : b + 1], l_half[b][:, 0:1], l_half[b][:, 1:2], 2.0, ADD, MULT)
+            nc.gpsimd.tensor_scalar(l_sum[b][:], l_half[b][:, 0:1], l_half[b][:, 1:2], 2.0, ADD, MULT)
 
-        def invert_sums():
-            nc.vector.reciprocal(inv_l[:], l_sum[:])
+        def invert_sum(b):
+            nc.vector.reciprocal(inv_l[b][:], l_sum[b][:])
 
-        def turn_values(b, w):
-            bank["v", b, w] = psum.tile([P, 4, P], F32, name="bank", tag=f"bank{(3, 1, 2, 6)[2 * b + w]}")
-            words = kb[b][:].rearrange("p n t -> p (n t)").bitcast(F32).rearrange("p (j s w) -> p w j s", j=4, w=2)
-            for j in range(4):
-                nc.tensor.transpose(bank["v", b, w][:, j, :], words[:, w, j, :], ident[:])
+        def turn_values(b, t):
+            u = t // 2
+            if t % 2 == 0:
+                bank["v", b, u] = psum.tile([P, 4, P], F32, name="bank", tag=f"bank{(6, 7, 4, 1)[2 * b + u]}")
+            words = planes[b][:, t * N : (t + 1) * N].bitcast(F32).rearrange("p (s h) -> p h s", h=2)
+            for h in range(2):
+                nc.tensor.transpose(bank["v", b, u][:, 2 * (t % 2) + h, :], words[:, h, :], ident[:])
 
-        def copy_values(b, w):
-            src = bank["v", b, w][:].rearrange("s j p -> s (j p)").bitcast(BF16).rearrange("s (j p e) -> s p j e", j=4, e=2)
-            nc.scalar.activation(out=vb[b][:].rearrange("s (p w e) j -> s w p j e", w=2, e=2)[:, w], in_=src, func=COPY)
+        def copy_values(b, u):
+            dst = vb[b][:].bitcast(F32).rearrange("s (p u w) -> s u p w", u=2, w=4)[:, u]
+            nc.scalar.copy(out=dst, in_=bank["v", b, u][:].rearrange("s w p -> s p w"))
 
         def turn_weights(b):
-            bank["w", b] = psum.tile([P, 4, P], F32, name="bank", tag=f"bank{4 + b}")
+            bank["w", b] = psum.tile([P, 4, P], F32, name="bank", tag=f"bank{(7, 4)[b]}")
             for j in range(4):
                 nc.tensor.transpose(bank["w", b][:, j, :], p[b][:, j, :], ident[:])
 
         def scale_weights(b):
-            wb[b] = keep.tile([P, NQ, 4], BF16, name="wb", tag=("wb0", "wb1")[b], align_bytes=64)
             nc.vector.tensor_tensor(
                 wb[b][:].rearrange("s (q i) j -> s q j i", i=2),
                 bank["w", b][:].rearrange("s j (q i) -> s q j i", i=2),
@@ -257,14 +232,17 @@ def tile_attend_x_mla_gate_seg_kernel(tc, qT, cT, ts, ch, og, offs, out):
                 stop=True,
             )
 
+        def take_middle():
+            middle = new([P, D + 8], F32, "middle", tag="win03")
+            gate[0] = middle[:, 0:D]
+            ts_col[1] = middle[:, D : D + 4].unsqueeze(2)
+
         def take_late():
-            late = keep.tile([P, 8 * N + 8], F32, name="late", tag="raw111", align_bytes=64)
-            for b in range(B):
-                vb[b] = late[:, 2 * N * b : 2 * N * (b + 1)].bitcast(BF16).rearrange("s (c j) -> s c j", j=4)
-                th[b] = late[:, (5 + b) * N : (6 + b) * N]
-            ts_rows[1] = late[:, 7 * N : 8 * N]
-            neg_m[0] = late[:, 8 * N : 8 * N + 1]
-            p[0] = late[:, 4 * N : 5 * N].rearrange("q (j s) -> q j s", j=4)
+            late = new([P, N + 2 * D + 16], F32, "late", tag="win13")
+            vb[1] = late[:, 0 : 2 * D].bitcast(BF16)
+            p[0] = late[:, 2 * D : 2 * D + N].rearrange("q (j s) -> q j s", j=4)
+            neg_m[0] = late[:, 2 * D + N : 2 * D + N + 1]
+            v_codes[0] = new([P, D], U32, "v_codes0", tag="win12")
 
         def gate_tanh(b):
             nc.scalar.activation(out=th[b][:], in_=og_sb[b][:], func=TANH, scale=0.5)
@@ -281,94 +259,107 @@ def tile_attend_x_mla_gate_seg_kernel(tc, qT, cT, ts, ch, og, offs, out):
 
         def finish(b, cols):
             y = bank["y", b, cols.start]
-            nc.vector.scalar_tensor_tensor(out=o[b][:, cols], in0=y[:], scalar=inv_l[:, b : b + 1], in1=gate[b][:, cols], op0=MULT, op1=MULT)
+            nc.vector.scalar_tensor_tensor(out=o[b][:, cols], in0=y[:], scalar=inv_l[b][:], in1=gate[b][:, cols], op0=MULT, op1=MULT)
             nc.sync.dma_start(out=out[b][:, cols], in_=o[b][:, cols])
 
-        load_pair(0, 0, 0)
+        load_plane(0, 0)
         nc.sync.dma_start(offsets[:], offs)
         load_scales(0)
-        load_pair(0, 0, 1)
-        load_scales(1)
-        load_pair(0, 1, 0)
-        load_pair(0, 1, 1)
         load_queries(0)
-        load_pair(1, 0, 0)
-        load_pair(1, 0, 1)
-        load_pair(1, 1, 0)
-        load_pair(1, 1, 1)
-        load_queries(1)
+        load_plane(0, 1)
+        load_scales(1)
         load_gate(0)
         load_channels()
+        load_plane(0, 2)
+        load_plane(0, 3)
+        load_plane(1, 0)
+        load_plane(1, 1)
+        load_queries(1)
+        load_plane(1, 2)
+        load_plane(1, 3)
         load_gate(1)
         nc.vector.memset(ident[:], 0.0)
         make_identity(nc, ident[:], nomemset=True)
         preload_exp()
         gather_scales(0)
         gather_scales(1)
-        cast(nc.scalar, 0, 0, 0)
-        cast(nc.scalar, 0, 0, 1)
-        cast(nc.scalar, 0, 1, 0)
-        cast(nc.scalar, 0, 1, 1)
-        turn_scales(0)
-        turn_scales(1)
-        gather_pair(0, 0)
-        scale_column(0)
-        scale_column(1)
-        spread_scales(1)
-        turn_values(0, 0)
+        gather_plane(nc.scalar, 0, 0)
+        gather_plane(nc.scalar, 0, 1)
         cast_queries(0)
         quantise_queries(0)
-        gather_pair(0, 1)
-        cast(nc.scalar, 1, 0, 0)
-        cast(nc.scalar, 1, 0, 1)
-        quantise_keys(0, ALL)
-        scores(0)
-        turn_values(0, 1)
-        gather_pair(1, 0)
-        cast(nc.scalar, 1, 1, 0)
-        cast(nc.scalar, 1, 1, 1)
-        take_late()
-        scale_scores(0)
-        cast_queries(1)
-        gather_pair(1, 1)
-        turn_values(1, 0)
-        turn_scores(0)
-        copy_spread(1)
-        copy_values(0, 0)
+        turn_scales(0)
+        turn_scales(1)
         spread_channels()
+        ts_col[0] = new([P, 4, 1], F32, "ts_col0", tag="win01")
+        scale_column(0)
+        gate_tanh(0)
+        gather_plane(nc.scalar, 0, 2, LEFT)
+        gather_plane(nc.vector, 0, 2, RIGHT)
+        gather_plane(nc.scalar, 0, 3, LEFT)
+        gather_plane(nc.vector, 0, 3, RIGHT)
+        take_middle()
+        scale_column(1)
+        weave(nc.vector, 0, EVERY)
+        gate_channels(0)
+        turn_values(0, 0)
+        turn_values(0, 1)
+        turn_values(0, 2)
+        turn_values(0, 3)
+        gather_plane(nc.scalar, 1, 0)
+        gather_plane(nc.scalar, 1, 1)
+        vb[0] = new([P, 4 * D], BF16, "vb0", tag="win10")
+        copy_values(0, 0)
         copy_values(0, 1)
+        quantise_keys(0, ALL)
+        scores(0, EVERY, "bank4")
+        scale_scores(0)
+        turn_scores(0, EVERY)
+        cast_queries(1)
         quantise_queries(1)
+        turn_values(1, 0)
+        turn_values(1, 1)
+        gather_plane(nc.scalar, 1, 2, LEFT)
+        gather_plane(nc.vector, 1, 2, RIGHT)
+        gather_plane(nc.scalar, 1, 3, LEFT)
+        gather_plane(nc.vector, 1, 3, RIGHT)
+        take_late()
+        weave(nc.vector, 1, LOW)
+        weave(nc.scalar, 1, HIGH)
+        maximum(0)
         quantise_keys(1, LEFT)
         quantise_keys(1, RIGHT)
-        row_scores(1, LEFT)
-        row_scores(1, RIGHT)
-        maximum(0)
-        copy_values(1, 0)
+        scores(1, LOW, "bank2")
+        scores(1, HIGH, "bank6")
         exponentials(0)
         add_sums(0)
-        scale_row_scores(1, LEFT)
-        scale_row_scores(1, RIGHT)
-        turn_values(1, 1)
-        turn_weights(0)
-        quantise_values(0)
+        scale_block(1, 0)
+        scale_block(1, 1)
+        scale_block(1, 2)
+        scale_block(1, 3)
+        turn_scores(1, LOW)
+        turn_scores(1, HIGH)
         maximum(1)
-        gate_tanh(0)
         exponentials(1)
         add_sums(1)
+        turn_values(1, 2)
+        turn_values(1, 3)
+        turn_weights(0)
+        quantise_values(0)
+        copy_values(1, 0)
         copy_values(1, 1)
-        scale_weights(0)
-        turn_weights(1)
         gate_tanh(1)
-        gate_channels(0)
+        turn_weights(1)
+        scale_weights(0)
+        invert_sum(0)
         quantise_weights(0)
         products(0, ALL)
         scale_weights(1)
-        invert_sums()
         quantise_values(1)
         quantise_weights(1)
         products(1, LEFT)
         products(1, RIGHT)
-        gate_channels(1)
+        invert_sum(1)
         finish(0, ALL)
+        gate_channels(1)
         finish(1, LEFT)
         finish(1, RIGHT)

@@ -58,18 +58,18 @@ def tile_attend_x_mla_gate_seg_kernel(tc, qT, cT, ts, ch, og, offs, out):
         q_bf = each([P, NQ, 4], BF16, "q_bf")
         q_codes, q_scales = each([P, NQ], U32, "q_codes"), each([P, NQ], U8, "q_scales")
         tsg = each([P, N], F32, "tsg")
-        ts_col, neg_m, p, vb = {}, {}, {}, {}
+        ts_col, ts_rows, neg_m, p, vb = {}, {}, {}, {}, {}
         a_t = each([P, 4, P], F32, "a_t")
         neg_m[1] = new([P, 1], F32, "neg_m1")
         p[1] = new([P, 4, P], F32, "p1")
         l_half = each([P, 2], F32, "l_half")
         l_sum = each([P, 1], F32, "l_sum")
         inv_l = each([P, 1], F32, "inv_l")
-        v_codes, v_scales = {1: new([P, D], U32, "v_codes1")}, each([P, D], U8, "v_scales")
+        v_codes, v_scales = each([P, D], U32, "v_codes"), each([P, D], U8, "v_scales")
         wb = each([P, NQ, 4], BF16, "wb")
         w_codes, w_scales = each([P, NQ], U32, "w_codes"), each([P, NQ], U8, "w_scales")
         th = each([P, D], F32, "th")
-        gate = {1: new([P, D], F32, "gate1")}
+        gate = each([P, D], F32, "gate")
         o = each([P, D], F32, "o")
         bank = {}
 
@@ -171,6 +171,32 @@ def tile_attend_x_mla_gate_seg_kernel(tc, qT, cT, ts, ch, og, offs, out):
         def scale_scores(b):
             nc.vector.tensor_tensor(a_t[b][:], bank["score", b][:], ts_col[b][:].to_broadcast([P, 4, NQ]), MULT)
 
+        def spread_scales(b):
+            bank["tsb", b] = psum.tile([P, 4, P], F32, name="bank", tag="bank5")
+            for j in range(4):
+                nc.tensor.transpose(bank["tsb", b][:, j, :], ts_col[b][:, j, :].to_broadcast([P, P]), ident[:])
+
+        def copy_spread(b):
+            nc.scalar.activation(out=ts_rows[b][:], in_=bank["tsb", b][:].rearrange("q j s -> q (j s)"), func=COPY)
+
+        def row_scores(b, cols):
+            tile = psum.tile([P, cols.stop - cols.start], F32, name="bank", tag=("bank2", "bank6")[cols.start // 256])
+            bank["score", b, cols.start] = tile
+            nc.tensor.matmul_mx(
+                out=tile[:],
+                lhsT=q_codes[b][:].bitcast(FP8X4),
+                lhsT_scale=q_scales[b][:],
+                rhs=k_codes[b][:, cols].bitcast(FP8X4),
+                rhs_scale=k_scales[b][:, cols],
+                start=True,
+                stop=True,
+            )
+
+        def scale_row_scores(b, cols):
+            flat = a_t[b][:].rearrange("q j s -> q (j s)")
+            nc.vector.tensor_tensor(flat[:, cols], bank["score", b, cols.start][:], ts_rows[b][:, cols], MULT)
+            bank["a", b] = a_t[b]
+
         def scale_block(b, j):
             nc.scalar.activation(out=a_t[b][:, j, :], in_=bank["score", b, j], func=COPY, scale=ts_col[b][:, j, :])
 
@@ -233,16 +259,15 @@ def tile_attend_x_mla_gate_seg_kernel(tc, qT, cT, ts, ch, og, offs, out):
             )
 
         def take_middle():
-            middle = new([P, D + 8], F32, "middle", tag="win03")
-            gate[0] = middle[:, 0:D]
-            ts_col[1] = middle[:, D : D + 4].unsqueeze(2)
+            middle = new([P, 2 * D + N], F32, "middle", tag="win03")
+            vb[0] = middle[:, 0 : 2 * D].bitcast(BF16)
+            ts_rows[1] = middle[:, 2 * D : 2 * D + N]
 
         def take_late():
             late = new([P, N + 2 * D + 16], F32, "late", tag="win13")
             vb[1] = late[:, 0 : 2 * D].bitcast(BF16)
             p[0] = late[:, 2 * D : 2 * D + N].rearrange("q (j s) -> q j s", j=4)
             neg_m[0] = late[:, 2 * D + N : 2 * D + N + 1]
-            v_codes[0] = new([P, D], U32, "v_codes0", tag="win12")
 
         def gate_tanh(b):
             nc.scalar.activation(out=th[b][:], in_=og_sb[b][:], func=TANH, scale=0.5)
@@ -258,25 +283,25 @@ def tile_attend_x_mla_gate_seg_kernel(tc, qT, cT, ts, ch, og, offs, out):
             )
 
         def finish(b, cols):
-            y = bank["y", b, cols.start]
-            nc.vector.scalar_tensor_tensor(out=o[b][:, cols], in0=y[:], scalar=inv_l[b][:], in1=gate[b][:, cols], op0=MULT, op1=MULT)
+            y = bank["y", b, cols.start][:] if b else bank["y", b, 0][:, cols]
+            nc.vector.scalar_tensor_tensor(out=o[b][:, cols], in0=y, scalar=inv_l[b][:], in1=gate[b][:, cols], op0=MULT, op1=MULT)
             nc.sync.dma_start(out=out[b][:, cols], in_=o[b][:, cols])
 
         load_plane(0, 0)
         nc.sync.dma_start(offsets[:], offs)
         load_scales(0)
-        load_queries(0)
         load_plane(0, 1)
         load_scales(1)
-        load_gate(0)
-        load_channels()
         load_plane(0, 2)
         load_plane(0, 3)
+        load_queries(0)
         load_plane(1, 0)
         load_plane(1, 1)
-        load_queries(1)
         load_plane(1, 2)
         load_plane(1, 3)
+        load_queries(1)
+        load_gate(0)
+        load_channels()
         load_gate(1)
         nc.vector.memset(ident[:], 0.0)
         make_identity(nc, ident[:], nomemset=True)
@@ -285,81 +310,82 @@ def tile_attend_x_mla_gate_seg_kernel(tc, qT, cT, ts, ch, og, offs, out):
         gather_scales(1)
         gather_plane(nc.scalar, 0, 0)
         gather_plane(nc.scalar, 0, 1)
-        cast_queries(0)
-        quantise_queries(0)
         turn_scales(0)
         turn_scales(1)
-        spread_channels()
         ts_col[0] = new([P, 4, 1], F32, "ts_col0", tag="win01")
         scale_column(0)
-        gate_tanh(0)
         gather_plane(nc.scalar, 0, 2, LEFT)
         gather_plane(nc.vector, 0, 2, RIGHT)
+        ts_col[1] = new([P, 4, 1], F32, "ts_col1", tag="win02")
+        scale_column(1)
         gather_plane(nc.scalar, 0, 3, LEFT)
         gather_plane(nc.vector, 0, 3, RIGHT)
         take_middle()
-        scale_column(1)
-        weave(nc.vector, 0, EVERY)
-        gate_channels(0)
         turn_values(0, 0)
         turn_values(0, 1)
+        spread_scales(1)
         turn_values(0, 2)
         turn_values(0, 3)
+        cast_queries(0)
+        weave(nc.vector, 0, LOW)
+        weave(nc.vector, 0, HIGH)
+        quantise_queries(0)
         gather_plane(nc.scalar, 1, 0)
         gather_plane(nc.scalar, 1, 1)
-        vb[0] = new([P, 4 * D], BF16, "vb0", tag="win10")
         copy_values(0, 0)
+        copy_spread(1)
         copy_values(0, 1)
-        quantise_keys(0, ALL)
+        quantise_keys(0, LEFT)
+        quantise_keys(0, RIGHT)
         scores(0, EVERY, "bank4")
         scale_scores(0)
+        quantise_values(0)
         turn_scores(0, EVERY)
-        cast_queries(1)
-        quantise_queries(1)
         turn_values(1, 0)
         turn_values(1, 1)
         gather_plane(nc.scalar, 1, 2, LEFT)
         gather_plane(nc.vector, 1, 2, RIGHT)
-        gather_plane(nc.scalar, 1, 3, LEFT)
-        gather_plane(nc.vector, 1, 3, RIGHT)
+        gather_plane(nc.scalar, 1, 3, slice(0, 128))
+        gather_plane(nc.vector, 1, 3, slice(128, 512))
         take_late()
+        cast_queries(1)
         weave(nc.vector, 1, LOW)
         weave(nc.scalar, 1, HIGH)
         maximum(0)
+        quantise_queries(1)
         quantise_keys(1, LEFT)
         quantise_keys(1, RIGHT)
-        scores(1, LOW, "bank2")
-        scores(1, HIGH, "bank6")
+        row_scores(1, LEFT)
+        row_scores(1, RIGHT)
         exponentials(0)
         add_sums(0)
-        scale_block(1, 0)
-        scale_block(1, 1)
-        scale_block(1, 2)
-        scale_block(1, 3)
-        turn_scores(1, LOW)
-        turn_scores(1, HIGH)
+        scale_row_scores(1, LEFT)
+        scale_row_scores(1, RIGHT)
         maximum(1)
         exponentials(1)
         add_sums(1)
         turn_values(1, 2)
         turn_values(1, 3)
         turn_weights(0)
-        quantise_values(0)
+        spread_channels()
+        gate_tanh(0)
         copy_values(1, 0)
         copy_values(1, 1)
         gate_tanh(1)
         turn_weights(1)
         scale_weights(0)
-        invert_sum(0)
+        gate_channels(0)
         quantise_weights(0)
         products(0, ALL)
-        scale_weights(1)
         quantise_values(1)
+        scale_weights(1)
+        invert_sum(0)
+        finish(0, LEFT)
         quantise_weights(1)
         products(1, LEFT)
         products(1, RIGHT)
-        invert_sum(1)
-        finish(0, ALL)
+        finish(0, RIGHT)
         gate_channels(1)
+        invert_sum(1)
         finish(1, LEFT)
         finish(1, RIGHT)

@@ -29,7 +29,11 @@ D = 512
 NQ = 128
 LIST = N // 16
 ALL, LEFT, RIGHT = slice(0, N), slice(0, N // 2), slice(N // 2, N)
-EVERY, LOW, HIGH = slice(0, 4), slice(0, 2), slice(2, 4)
+SHARE = 128
+
+
+def chunk(c, n=1):
+    return slice(c * P, (c + n) * P)
 
 
 def tile_attend_x_mla_gate_seg_kernel(tc, qT, cT, ts, ch, og, offs, out):
@@ -37,6 +41,7 @@ def tile_attend_x_mla_gate_seg_kernel(tc, qT, cT, ts, ch, og, offs, out):
     with ExitStack() as ctx:
         lists = ctx.enter_context(tc.tile_pool(name="lists", bufs=1))
         keep = ctx.enter_context(tc.tile_pool(name="keep", bufs=1))
+        laid = ctx.enter_context(tc.tile_pool(name="laid", bufs=1))
         psum = ctx.enter_context(tc.psum_pool(name="psum", bufs=1))
 
         offsets = lists.tile([P, B * LIST], U16, name="offsets")
@@ -44,13 +49,20 @@ def tile_attend_x_mla_gate_seg_kernel(tc, qT, cT, ts, ch, og, offs, out):
         def new(shape, dtype, name, tag=None):
             return keep.tile(shape, dtype, name=name, tag=tag or name, align_bytes=64)
 
+        def lay(shape, dtype, name, offset):
+            return laid.tile(shape, dtype, name=name, align_bytes=64, offset=offset)
+
         def each(shape, dtype, name):
             return [new(shape, dtype, f"{name}{b}") for b in range(B)]
 
+        def new_bank(number, columns=N):
+            return psum.tile([P, columns], F32, name="bank", tag=f"bank{number}")
+
         win = {(b, t): new([P, (b + 1) * SEG], F32, f"win{b}{t}") for b in range(B) for t in range(4)}
         scale_tab = new([P, T], F32, "scale_tab")
-        q_raw = each([P, 4, NQ], F32, "q_raw")
+        q_raw = [new([P, 4, NQ], F32, "q_raw0"), lay([P, 4, NQ], F32, "q_raw1", 0)]
         ch_col = new([P, 4], F32, "ch_col")
+        ch_half = new([P, 4], F32, "ch_half")
         og_sb = each([P, D], F32, "og_sb")
         planes = each([P, 4 * N], BF16, "planes")
         kb = each([P, 4 * N], BF16, "kb")
@@ -58,19 +70,20 @@ def tile_attend_x_mla_gate_seg_kernel(tc, qT, cT, ts, ch, og, offs, out):
         q_bf = each([P, NQ, 4], BF16, "q_bf")
         q_codes, q_scales = each([P, NQ], U32, "q_codes"), each([P, NQ], U8, "q_scales")
         tsg = each([P, N], F32, "tsg")
-        ts_col, ts_rows, neg_m, p, vb = {}, {}, {}, {}, {}
+        ts_col, ts_rows = {}, {}
+        neg_m, p = {}, {}
         a_t = each([P, 4, P], F32, "a_t")
         neg_m[1] = new([P, 1], F32, "neg_m1")
         p[1] = new([P, 4, P], F32, "p1")
-        l_half = each([P, 2], F32, "l_half")
-        l_sum = each([P, 1], F32, "l_sum")
-        inv_l = each([P, 1], F32, "inv_l")
-        v_codes, v_scales = each([P, D], U32, "v_codes"), each([P, D], U8, "v_scales")
-        wb = each([P, NQ, 4], BF16, "wb")
+        l_part = new([P, 2], F32, "l_part")
+        l_sum = new([P, B], F32, "l_sum")
+        inv_l = new([P, B], F32, "inv_l")
+        vb, wb, gate, o = {}, {}, {}, {}
+        v_codes, v_scales = each([P, D], U32, "v_codes"), {0: new([P, D], U8, "v_scales0")}
+        wb[1] = new([P, NQ, 4], BF16, "wb1")
+        o[1] = new([P, D], F32, "o1")
         w_codes, w_scales = each([P, NQ], U32, "w_codes"), each([P, NQ], U8, "w_scales")
         th = each([P, D], F32, "th")
-        gate = each([P, D], F32, "gate")
-        o = each([P, D], F32, "o")
         bank = {}
 
         ident = new([P, P], F32, "ident")
@@ -97,9 +110,10 @@ def tile_attend_x_mla_gate_seg_kernel(tc, qT, cT, ts, ch, og, offs, out):
             nc.sync.dma_start(out=ch_col[:], in_=ch[0].rearrange("(p t) -> p t", t=4))
 
         def spread_channels():
-            bank["ch"] = psum.tile([P, 4, P], F32, name="bank", tag="bank3")
+            nc.vector.tensor_scalar(ch_half[:], ch_col[:], 0.5, None, MULT)
+            bank["ch"] = new_bank(0)
             for t in range(4):
-                nc.tensor.transpose(bank["ch"][:, t, :], ch_col[:, t : t + 1].to_broadcast([P, P]), ident[:])
+                nc.tensor.transpose(bank["ch"][:, chunk(t)], ch_half[:, t : t + 1].to_broadcast([P, P]), ident[:])
 
         def load_gate(b):
             nc.sync.dma_start(out=og_sb[b][:], in_=og[b])
@@ -112,9 +126,10 @@ def tile_attend_x_mla_gate_seg_kernel(tc, qT, cT, ts, ch, og, offs, out):
             else:
                 nc.vector.tensor_copy(out=dst, in_=src)
 
-        def weave(engine, b, js):
-            dst = kb[b][:].rearrange("p (j c i t) -> p c t i j", j=4, i=2, t=4)[:, :, :, :, js]
-            src = planes[b][:].rearrange("p (t c i j) -> p c t i j", t=4, i=2, j=4)[:, :, :, :, js]
+        def weave(b, cols, engine=nc.vector):
+            quads = slice(cols.start // 4, cols.stop // 4)
+            dst = kb[b][:].rearrange("p (c i t) -> p c t i", i=4, t=4)[:, quads]
+            src = planes[b][:].rearrange("p (t c i) -> p c t i", t=4, i=4)[:, quads]
             if engine is nc.scalar:
                 nc.scalar.copy(out=dst, in_=src)
             else:
@@ -124,18 +139,36 @@ def tile_attend_x_mla_gate_seg_kernel(tc, qT, cT, ts, ch, og, offs, out):
             window = scale_tab[:].bitcast(U32)
             if b == 0:
                 window = window[:, 0:SEG]
-            nc.vector.tensor_copy(tsg[b][:].bitcast(U32).rearrange("p (j s) -> p s j", j=4), window.indirect(offsets[:, b * LIST : (b + 1) * LIST]))
+            nc.vector.tensor_copy(tsg[b][:].bitcast(U32), window.indirect(offsets[:, b * LIST : (b + 1) * LIST]))
 
         def turn_scales(b):
-            bank["ts", b] = psum.tile([P, 4, P], F32, name="bank", tag=f"bank{2 - b}")
+            bank["ts", b] = new_bank(1, P + 8)
             for j in range(4):
-                nc.tensor.transpose(bank["ts", b][:, j, :], tsg[b][:, j * P : (j + 1) * P], ident[:])
+                nc.tensor.transpose(bank["ts", b][:, 2 * j : 2 * j + P], tsg[b][:].rearrange("p (s j) -> p j s", j=4)[:, j, :], ident[:])
 
-        def scale_column(b):
-            nc.scalar.activation(out=ts_col[b][:], in_=bank["ts", b][:, :, 0:1], func=COPY)
+        def copy(engine, dst, src):
+            if engine is nc.scalar:
+                nc.scalar.activation(out=dst, in_=src, func=COPY)
+            else:
+                nc.vector.tensor_copy(out=dst, in_=src)
+
+        def scale_columns(engine, b):
+            copy(engine, ts_col[b][:], bank["ts", b][:, 0:8].rearrange("p (k e) -> p k e", e=2)[:, :, 0])
+
+        def spread_scales(b):
+            bank["tsb", b] = new_bank((5, 3)[b])
+            for j in range(4):
+                nc.tensor.transpose(bank["tsb", b][:, chunk(j)], ts_col[b][:, j : j + 1].to_broadcast([P, P]), ident[:])
+
+        def scale_rows(engine, b):
+            copy(engine, ts_rows[b][:].rearrange("q j s -> q (j s)"), bank["tsb", b][:])
 
         def cast_queries(b):
-            nc.gpsimd.tensor_scalar(q_bf[b][:], q_raw[b][:].rearrange("p t q -> p q t"), 1.0, 0.0, MULT, ADD)
+            if b == 0:
+                nc.gpsimd.tensor_scalar(q_bf[b][:], q_raw[b][:].rearrange("p t q -> p q t"), 1.0, 0.0, MULT, ADD)
+            else:
+                dst = q_bf[b][:].rearrange("p (c i) t -> p c t i", i=4)
+                nc.scalar.activation(out=dst, in_=q_raw[b][:].rearrange("p t (c i) -> p c t i", i=4), func=COPY)
 
         def quantise(codes, scales, src):
             nc.vector.quantize_mx(out=codes.bitcast(FP8X4), scales=scales, in_=src)
@@ -146,41 +179,14 @@ def tile_attend_x_mla_gate_seg_kernel(tc, qT, cT, ts, ch, og, offs, out):
         def quantise_keys(b, cols):
             quantise(k_codes[b][:, cols], k_scales[b][:, cols], kb[b][:, 4 * cols.start : 4 * cols.stop])
 
-        def quantise_values(b):
-            quantise(v_codes[b][:], v_scales[b][:], vb[b][:])
+        def quantise_values(b, cols=ALL):
+            quantise(v_codes[b][:, cols], v_scales[b][:, cols], vb[b, cols.start // 256][:] if b == 0 else vb[b][:])
 
-        def quantise_weights(b):
-            quantise(w_codes[b][:], w_scales[b][:], wb[b][:].rearrange("p n t -> p (n t)"))
+        def quantise_weights(b, rows=slice(0, NQ)):
+            quantise(w_codes[b][:, rows], w_scales[b][:, rows], wb[b][:, rows].rearrange("p n t -> p (n t)"))
 
-        def scores(b, js, tag):
-            tile = psum.tile([P, js.stop - js.start, NQ], F32, name="bank", tag=tag)
-            for j in range(js.start, js.stop):
-                bank["score", b, j] = tile[:, j - js.start, :]
-                cols = slice(j * P, (j + 1) * P)
-                nc.tensor.matmul_mx(
-                    out=bank["score", b, j],
-                    lhsT=k_codes[b][:, cols].bitcast(FP8X4),
-                    lhsT_scale=k_scales[b][:, cols],
-                    rhs=q_codes[b][:].bitcast(FP8X4),
-                    rhs_scale=q_scales[b][:],
-                    start=True,
-                    stop=True,
-                )
-            bank["score", b] = tile
-
-        def scale_scores(b):
-            nc.vector.tensor_tensor(a_t[b][:], bank["score", b][:], ts_col[b][:].to_broadcast([P, 4, NQ]), MULT)
-
-        def spread_scales(b):
-            bank["tsb", b] = psum.tile([P, 4, P], F32, name="bank", tag="bank5")
-            for j in range(4):
-                nc.tensor.transpose(bank["tsb", b][:, j, :], ts_col[b][:, j, :].to_broadcast([P, P]), ident[:])
-
-        def copy_spread(b):
-            nc.scalar.activation(out=ts_rows[b][:], in_=bank["tsb", b][:].rearrange("q j s -> q (j s)"), func=COPY)
-
-        def row_scores(b, cols):
-            tile = psum.tile([P, cols.stop - cols.start], F32, name="bank", tag=("bank2", "bank6")[cols.start // 256])
+        def scores(b, cols, number):
+            tile = new_bank(number, cols.stop - cols.start)
             bank["score", b, cols.start] = tile
             nc.tensor.matmul_mx(
                 out=tile[:],
@@ -192,61 +198,56 @@ def tile_attend_x_mla_gate_seg_kernel(tc, qT, cT, ts, ch, og, offs, out):
                 stop=True,
             )
 
-        def scale_row_scores(b, cols):
-            flat = a_t[b][:].rearrange("q j s -> q (j s)")
-            nc.vector.tensor_tensor(flat[:, cols], bank["score", b, cols.start][:], ts_rows[b][:, cols], MULT)
-            bank["a", b] = a_t[b]
-
-        def scale_block(b, j):
-            nc.scalar.activation(out=a_t[b][:, j, :], in_=bank["score", b, j], func=COPY, scale=ts_col[b][:, j, :])
-
-        def turn_scores(b, js):
-            if js.start == 0:
-                bank["a", b] = psum.tile([P, 4, P], F32, name="bank", tag=("bank0", "bank5")[b])
-            for j in range(js.start, js.stop):
-                nc.tensor.transpose(bank["a", b][:, j, :], a_t[b][:, j, :], ident[:])
+        def scale_scores(b, cols):
+            rows = slice(cols.start // 4, cols.stop // 4)
+            src = bank["score", b, cols.start][:].rearrange("q (s j) -> q j s", j=4)
+            nc.vector.tensor_tensor(a_t[b][:, :, rows], src, ts_rows[b][:, :, rows], MULT)
 
         def maximum(b):
-            nc.vector.tensor_reduce(out=neg_m[b][:], in_=bank["a", b][:].rearrange("q j s -> q (j s)"), axis=AXIS_X, op=MAX, negate=True)
+            nc.vector.tensor_reduce(out=neg_m[b][:], in_=a_t[b][:].rearrange("q j s -> q (j s)"), axis=AXIS_X, op=MAX, negate=True)
 
-        def exponentials(b):
-            for h in range(2):
-                j2 = slice(2 * h, 2 * h + 2)
-                nc.scalar.activation(out=p[b][:, j2], in_=bank["a", b][:, j2], func=EXP, bias=neg_m[b][:], accum_out=l_half[b][:, h : h + 1])
+        def exponentials(b, js, total):
+            nc.scalar.activation(out=p[b][:, js], in_=a_t[b][:, js], func=EXP, bias=neg_m[b][:], accum_out=total)
 
-        def add_sums(b):
-            nc.gpsimd.tensor_scalar(l_sum[b][:], l_half[b][:, 0:1], l_half[b][:, 1:2], 2.0, ADD, MULT)
+        def add_sums():
+            nc.vector.tensor_reduce(out=l_sum[:, 1:2], in_=l_part[:], axis=AXIS_X, op=ADD)
 
-        def invert_sum(b):
-            nc.vector.reciprocal(inv_l[b][:], l_sum[b][:])
+        def invert_sums():
+            nc.vector.reciprocal(inv_l[:], l_sum[:])
 
         def turn_values(b, t):
             u = t // 2
             if t % 2 == 0:
-                bank["v", b, u] = psum.tile([P, 4, P], F32, name="bank", tag=f"bank{(6, 7, 4, 1)[2 * b + u]}")
+                bank["v", b, u] = new_bank((3, 4, 2, 4)[2 * b + u])
             words = planes[b][:, t * N : (t + 1) * N].bitcast(F32).rearrange("p (s h) -> p h s", h=2)
             for h in range(2):
-                nc.tensor.transpose(bank["v", b, u][:, 2 * (t % 2) + h, :], words[:, h, :], ident[:])
+                nc.tensor.transpose(bank["v", b, u][:, chunk(2 * (t % 2) + h)], words[:, h, :], ident[:])
 
         def copy_values(b, u):
-            dst = vb[b][:].bitcast(F32).rearrange("s (p u w) -> s u p w", u=2, w=4)[:, u]
-            nc.scalar.copy(out=dst, in_=bank["v", b, u][:].rearrange("s w p -> s p w"))
+            if b == 0:
+                dst = vb[b, u][:].bitcast(F32).rearrange("s (t p h) -> s t p h", t=2, h=2)
+                nc.scalar.copy(out=dst, in_=bank["v", b, u][:].rearrange("s (t h p) -> s t p h", t=2, h=2))
+            else:
+                dst = vb[b][:].bitcast(F32).rearrange("s (p u w) -> s u p w", u=2, w=4)[:, u]
+                nc.scalar.copy(out=dst, in_=bank["v", b, u][:].rearrange("s (w p) -> s p w", w=4))
 
-        def turn_weights(b):
-            bank["w", b] = psum.tile([P, 4, P], F32, name="bank", tag=f"bank{(7, 4)[b]}")
-            for j in range(4):
-                nc.tensor.transpose(bank["w", b][:, j, :], p[b][:, j, :], ident[:])
+        def turn_weights(b, js):
+            if js.start == 0:
+                bank["w", b] = new_bank((6, 7)[b])
+            for j in range(js.start, js.stop):
+                nc.tensor.transpose(bank["w", b][:, chunk(j)], p[b][:, j, :], ident[:])
 
-        def scale_weights(b):
+        def scale_weights(b, rows=slice(0, NQ)):
+            pairs = slice(rows.start // 2, rows.stop // 2)
             nc.vector.tensor_tensor(
-                wb[b][:].rearrange("s (q i) j -> s q j i", i=2),
-                bank["w", b][:].rearrange("s j (q i) -> s q j i", i=2),
-                ts_col[b][:].unsqueeze(1).to_broadcast([P, NQ // 2, 4, 2]),
+                wb[b][:].rearrange("s (q i) j -> s q j i", i=2)[:, pairs],
+                bank["w", b][:].rearrange("s (j q i) -> s q j i", j=4, i=2)[:, pairs],
+                ts_col[b][:].unsqueeze(1).unsqueeze(3).to_broadcast([P, pairs.stop - pairs.start, 4, 2]),
                 MULT,
             )
 
-        def products(b, cols):
-            tile = psum.tile([P, cols.stop - cols.start], F32, name="bank", tag=f"bank{6 + cols.start // 256 if b else 0}")
+        def products(b, cols, number):
+            tile = new_bank(number, cols.stop - cols.start)
             bank["y", b, cols.start] = tile
             nc.tensor.matmul_mx(
                 out=tile[:],
@@ -258,17 +259,6 @@ def tile_attend_x_mla_gate_seg_kernel(tc, qT, cT, ts, ch, og, offs, out):
                 stop=True,
             )
 
-        def take_middle():
-            middle = new([P, 2 * D + N], F32, "middle", tag="win03")
-            vb[0] = middle[:, 0 : 2 * D].bitcast(BF16)
-            ts_rows[1] = middle[:, 2 * D : 2 * D + N]
-
-        def take_late():
-            late = new([P, N + 2 * D + 16], F32, "late", tag="win13")
-            vb[1] = late[:, 0 : 2 * D].bitcast(BF16)
-            p[0] = late[:, 2 * D : 2 * D + N].rearrange("q (j s) -> q j s", j=4)
-            neg_m[0] = late[:, 2 * D + N : 2 * D + N + 1]
-
         def gate_tanh(b):
             nc.scalar.activation(out=th[b][:], in_=og_sb[b][:], func=TANH, scale=0.5)
 
@@ -277,115 +267,135 @@ def tile_attend_x_mla_gate_seg_kernel(tc, qT, cT, ts, ch, og, offs, out):
                 out=gate[b][:].rearrange("q (p t) -> q p t", t=4),
                 in0=th[b][:].rearrange("q (p t) -> q p t", t=4),
                 scalar=1.0,
-                in1=bank["ch"][:].rearrange("q t p -> q p t"),
+                in1=bank["ch"][:].rearrange("q (t p) -> q p t", t=4),
                 op0=ADD,
                 op1=MULT,
             )
 
         def finish(b, cols):
-            y = bank["y", b, cols.start][:] if b else bank["y", b, 0][:, cols]
-            nc.vector.scalar_tensor_tensor(out=o[b][:, cols], in0=y, scalar=inv_l[b][:], in1=gate[b][:, cols], op0=MULT, op1=MULT)
+            y, dst, factor = bank["y", b, cols.start][:], o[b][:, cols], gate[b][:, cols]
+            if b == 0:
+                y = y.rearrange("q (t p) -> q p t", t=4)
+                dst, factor = dst.rearrange("q (p t) -> q p t", t=4), factor.rearrange("q (p t) -> q p t", t=4)
+            nc.vector.scalar_tensor_tensor(out=dst, in0=y, scalar=inv_l[:, b : b + 1], in1=factor, op0=MULT, op1=MULT)
             nc.sync.dma_start(out=out[b][:, cols], in_=o[b][:, cols])
 
         load_plane(0, 0)
         nc.sync.dma_start(offsets[:], offs)
+        load_channels()
         load_scales(0)
         load_plane(0, 1)
         load_scales(1)
         load_plane(0, 2)
-        load_plane(0, 3)
         load_queries(0)
-        load_plane(1, 0)
-        load_plane(1, 1)
-        load_plane(1, 2)
-        load_plane(1, 3)
+        load_plane(0, 3)
+        for t in range(4):
+            load_plane(1, t)
         load_queries(1)
         load_gate(0)
-        load_channels()
         load_gate(1)
         nc.vector.memset(ident[:], 0.0)
         make_identity(nc, ident[:], nomemset=True)
         preload_exp()
+        spread_channels()
         gather_scales(0)
-        gather_scales(1)
         gather_plane(nc.scalar, 0, 0)
+        gather_scales(1)
         gather_plane(nc.scalar, 0, 1)
+        turn_values(0, 0)
         turn_scales(0)
-        turn_scales(1)
-        ts_col[0] = new([P, 4, 1], F32, "ts_col0", tag="win01")
-        scale_column(0)
+        turn_values(0, 1)
         gather_plane(nc.scalar, 0, 2, LEFT)
         gather_plane(nc.vector, 0, 2, RIGHT)
-        ts_col[1] = new([P, 4, 1], F32, "ts_col1", tag="win02")
-        scale_column(1)
-        gather_plane(nc.scalar, 0, 3, LEFT)
-        gather_plane(nc.vector, 0, 3, RIGHT)
-        take_middle()
-        turn_values(0, 0)
-        turn_values(0, 1)
-        spread_scales(1)
-        turn_values(0, 2)
-        turn_values(0, 3)
         cast_queries(0)
-        weave(nc.vector, 0, LOW)
-        weave(nc.vector, 0, HIGH)
-        quantise_queries(0)
-        gather_plane(nc.scalar, 1, 0)
-        gather_plane(nc.scalar, 1, 1)
+        ts_col[0] = new([P, 4], F32, "ts_col0", tag="win01")
+        scale_columns(nc.vector, 0)
+        vb[0, 0] = new([P, 2 * D], BF16, "vb00", tag="win02")
         copy_values(0, 0)
-        copy_spread(1)
-        copy_values(0, 1)
+        spread_scales(0)
+        turn_values(0, 2)
+        turn_scales(1)
+        quantise_queries(0)
+        ts_rows[0] = new([P, 4, P], F32, "ts_rows0")
+        scale_rows(nc.vector, 0)
+        for c in range(4):
+            gather_plane(nc.scalar, 0, 3, chunk(c))
+        turn_values(0, 3)
+        for c in range(3):
+            weave(0, chunk(c))
         quantise_keys(0, LEFT)
+        weave(0, chunk(3))
+        quantise_values(0, LEFT)
         quantise_keys(0, RIGHT)
-        scores(0, EVERY, "bank4")
-        scale_scores(0)
-        quantise_values(0)
-        turn_scores(0, EVERY)
+        gather_plane(nc.scalar, 1, 0)
+        middle = new([P, D + 16], F32, "middle", tag="win10")
+        vb[0, 1] = middle[:, 0:D].bitcast(BF16)
+        ts_col[1] = middle[:, D : D + 4]
+        copy_values(0, 1)
+        scale_columns(nc.scalar, 1)
+        gather_plane(nc.scalar, 1, 1)
+        scores(0, LEFT, 3)
+        scores(0, RIGHT, 2)
+        scale_scores(0, LEFT)
+        gather_plane(nc.vector, 1, 2, slice(SHARE, N))
+        scale_scores(0, RIGHT)
         turn_values(1, 0)
         turn_values(1, 1)
-        gather_plane(nc.scalar, 1, 2, LEFT)
-        gather_plane(nc.vector, 1, 2, RIGHT)
-        gather_plane(nc.scalar, 1, 3, slice(0, 128))
-        gather_plane(nc.vector, 1, 3, slice(128, 512))
-        take_late()
-        cast_queries(1)
-        weave(nc.vector, 1, LOW)
-        weave(nc.scalar, 1, HIGH)
+        spread_scales(1)
+        gather_plane(nc.scalar, 1, 2, slice(0, SHARE))
+        quantise_values(0, RIGHT)
+        neg_m[0] = new([P, 1], F32, "neg_m0")
         maximum(0)
-        quantise_queries(1)
-        quantise_keys(1, LEFT)
-        quantise_keys(1, RIGHT)
-        row_scores(1, LEFT)
-        row_scores(1, RIGHT)
-        exponentials(0)
-        add_sums(0)
-        scale_row_scores(1, LEFT)
-        scale_row_scores(1, RIGHT)
-        maximum(1)
-        exponentials(1)
-        add_sums(1)
+        for c in range(4):
+            gather_plane(nc.scalar, 1, 3, chunk(c))
         turn_values(1, 2)
         turn_values(1, 3)
-        turn_weights(0)
-        spread_channels()
+        cast_queries(1)
+        for c in range(3):
+            weave(1, chunk(c))
+        quantise_keys(1, LEFT)
+        weave(1, chunk(3))
+        quantise_queries(1)
+        quantise_keys(1, RIGHT)
         gate_tanh(0)
+        ts_rows[1] = lay([P, 4, P], F32, "ts_rows1", 0)
+        scale_rows(nc.scalar, 1)
+        late = new([P, N + 2 * D], F32, "late", tag="og_sb0")
+        p[0] = late[:, 0:N].rearrange("q (j s) -> q j s", j=4)
+        vb[1] = late[:, N : N + 2 * D].bitcast(BF16)
+        exponentials(0, slice(0, 4), l_sum[:, 0:1])
         copy_values(1, 0)
         copy_values(1, 1)
         gate_tanh(1)
-        turn_weights(1)
-        scale_weights(0)
+        gate[0] = new([P, D], F32, "gate0", tag="planes1")
         gate_channels(0)
-        quantise_weights(0)
-        products(0, ALL)
+        scores(1, LEFT, 6)
+        scores(1, RIGHT, 1)
+        scale_scores(1, LEFT)
+        turn_weights(0, slice(0, 4))
+        scale_scores(1, RIGHT)
+        maximum(1)
+        wb[0] = lay([P, NQ, 4], BF16, "wb0", 0)
+        v_scales[1] = lay([P, D], U8, "v_scales1", 1024)
+        gate[1] = lay([P, D], F32, "gate1", 1536)
+        scale_weights(0)
         quantise_values(1)
-        scale_weights(1)
-        invert_sum(0)
-        finish(0, LEFT)
-        quantise_weights(1)
-        products(1, LEFT)
-        products(1, RIGHT)
-        finish(0, RIGHT)
+        quantise_weights(0)
         gate_channels(1)
-        invert_sum(1)
+        for h in range(2):
+            js = slice(2 * h, 2 * h + 2)
+            exponentials(1, js, l_part[:, h : h + 1])
+            turn_weights(1, js)
+        products(0, ALL, 5)
+        add_sums()
+        scale_weights(1, slice(0, 64))
+        invert_sums()
+        scale_weights(1, slice(64, NQ))
+        quantise_weights(1, slice(0, 64))
+        quantise_weights(1, slice(64, NQ))
+        o[0] = new([P, D], F32, "o0", tag="win10")
+        finish(0, ALL)
+        products(1, LEFT, 3)
+        products(1, RIGHT, 1)
         finish(1, LEFT)
         finish(1, RIGHT)

@@ -29,7 +29,9 @@ D = 512
 NQ = 128
 LIST = N // 16
 ALL, LEFT, RIGHT = slice(0, N), slice(0, N // 2), slice(N // 2, N)
-SHARE = 128
+LOW, HIGH = slice(0, 2), slice(2, 4)
+SHARE = 288
+LAST_SHARE = 320
 
 
 def chunk(c, n=1):
@@ -60,9 +62,8 @@ def tile_attend_x_mla_gate_seg_kernel(tc, qT, cT, ts, ch, og, offs, out):
 
         win = {(b, t): new([P, (b + 1) * SEG], F32, f"win{b}{t}") for b in range(B) for t in range(4)}
         scale_tab = new([P, T], F32, "scale_tab")
-        q_raw = [new([P, 4, NQ], F32, "q_raw0"), lay([P, 4, NQ], F32, "q_raw1", 0)]
-        ch_col = new([P, 4], F32, "ch_col")
-        ch_half = new([P, 4], F32, "ch_half")
+        q_raw = [new([P, 4, NQ], F32, "q_raw0"), lay([P, 4, NQ], F32, "q_raw1", 6080)]
+        ch_sb = new([P, D], F32, "ch_sb")
         og_sb = each([P, D], F32, "og_sb")
         planes = each([P, 4 * N], BF16, "planes")
         kb = each([P, 4 * N], BF16, "kb")
@@ -70,20 +71,22 @@ def tile_attend_x_mla_gate_seg_kernel(tc, qT, cT, ts, ch, og, offs, out):
         q_bf = each([P, NQ, 4], BF16, "q_bf")
         q_codes, q_scales = each([P, NQ], U32, "q_codes"), each([P, NQ], U8, "q_scales")
         tsg = each([P, N], F32, "tsg")
-        ts_col, ts_rows = {}, {}
-        neg_m, p = {}, {}
+        ts_col = each([P, 4], F32, "ts_col")
+        ts_rows = {}
+        neg_m, p, vb = {}, {}, {}
         a_t = each([P, 4, P], F32, "a_t")
         neg_m[1] = new([P, 1], F32, "neg_m1")
         p[1] = new([P, 4, P], F32, "p1")
+        l_first = new([P, 1], F32, "l_first")
         l_part = new([P, 2], F32, "l_part")
-        l_sum = new([P, B], F32, "l_sum")
+        l_twice = new([P, B], F32, "l_twice")
         inv_l = new([P, B], F32, "inv_l")
-        vb, wb, gate, o = {}, {}, {}, {}
-        v_codes, v_scales = each([P, D], U32, "v_codes"), {0: new([P, D], U8, "v_scales0")}
-        wb[1] = new([P, NQ, 4], BF16, "wb1")
-        o[1] = new([P, D], F32, "o1")
+        v_codes, v_scales = each([P, D], U32, "v_codes"), {(0, 0): new([P, D // 2], U8, "v_scales00")}
+        wb = each([P, NQ, 4], BF16, "wb")
         w_codes, w_scales = each([P, NQ], U32, "w_codes"), each([P, NQ], U8, "w_scales")
-        th = each([P, D], F32, "th")
+        th, o = each([P, D], F32, "th"), each([P, D], F32, "o")
+        gate = {0: new([P, D], F32, "gate0")}
+        dealt = {}
         bank = {}
 
         ident = new([P, P], F32, "ident")
@@ -98,77 +101,70 @@ def tile_attend_x_mla_gate_seg_kernel(tc, qT, cT, ts, ch, og, offs, out):
             cols = slice(b * SEG, (b + 1) * SEG)
             nc.sync.dma_start(out=win[b, t][:, cols], in_=cT.rearrange("(p t) n -> p t n", t=4)[:, t, cols])
 
-        def load_scales(b):
-            cols = slice(b * SEG, (b + 1) * SEG)
-            nc.vector.memset(scale_tab[:, cols].bitcast(I32), 0)
-            nc.sync.dma_start(out=scale_tab[0:1, cols], in_=ts[0:1, cols])
+        def load_scales():
+            nc.scalar.dma_start(out=scale_tab[P - B : P, SEG:T], in_=ts[0].rearrange("(b n) -> b n", b=B))
+
+        def clear_scales():
+            nc.vector.memset(scale_tab[0 : P - B, SEG:T].bitcast(I32), 0)
 
         def load_queries(b):
             nc.sync.dma_start(out=q_raw[b][:], in_=qT[b].rearrange("(p t) q -> p t q", t=4))
 
         def load_channels():
-            nc.sync.dma_start(out=ch_col[:], in_=ch[0].rearrange("(p t) -> p t", t=4))
-
-        def spread_channels():
-            nc.vector.tensor_scalar(ch_half[:], ch_col[:], 0.5, None, MULT)
-            bank["ch"] = new_bank(0)
-            for t in range(4):
-                nc.tensor.transpose(bank["ch"][:, chunk(t)], ch_half[:, t : t + 1].to_broadcast([P, P]), ident[:])
+            nc.sync.dma_start(out=ch_sb[:], in_=ch)
 
         def load_gate(b):
             nc.sync.dma_start(out=og_sb[b][:], in_=og[b])
 
-        def gather_plane(engine, b, t, cols=ALL):
-            dst = planes[b][:, t * N + cols.start : t * N + cols.stop]
-            src = win[b, t][:].indirect(offsets[:, b * LIST + cols.start // 16 : b * LIST + cols.stop // 16])
+        def move(engine, dst, src):
             if engine is nc.scalar:
                 nc.scalar.activation(out=dst, in_=src, func=COPY)
             else:
                 nc.vector.tensor_copy(out=dst, in_=src)
 
-        def weave(b, cols, engine=nc.vector):
-            quads = slice(cols.start // 4, cols.stop // 4)
-            dst = kb[b][:].rearrange("p (c i t) -> p c t i", i=4, t=4)[:, quads]
-            src = planes[b][:].rearrange("p (t c i) -> p c t i", t=4, i=4)[:, quads]
+        def move_bits(engine, dst, src):
             if engine is nc.scalar:
                 nc.scalar.copy(out=dst, in_=src)
             else:
                 nc.vector.tensor_copy(out=dst, in_=src)
 
-        def gather_scales(b):
-            window = scale_tab[:].bitcast(U32)
-            if b == 0:
-                window = window[:, 0:SEG]
-            nc.vector.tensor_copy(tsg[b][:].bitcast(U32), window.indirect(offsets[:, b * LIST : (b + 1) * LIST]))
+        def gather_plane(engine, b, t, cols=ALL):
+            dst = planes[b][:, t * N + cols.start : t * N + cols.stop]
+            move(engine, dst, win[b, t][:].indirect(offsets[:, b * LIST + cols.start // 16 : b * LIST + cols.stop // 16]))
 
-        def turn_scales(b):
-            bank["ts", b] = new_bank(1, P + 8)
+        def gather_scales(engine, b):
+            window = scale_tab[:] if b else scale_tab[:, SEG:T]
+            move(engine, tsg[b][:], window.indirect(offsets[:, b * LIST : (b + 1) * LIST]))
+
+        def weave(engine, b, cols):
+            quads = slice(cols.start // 4, cols.stop // 4)
+            dst = kb[b][:].rearrange("p (c i t) -> p c t i", i=4, t=4)[:, quads]
+            src = planes[b][:].rearrange("p (t c i) -> p c t i", t=4, i=4)[:, quads]
+            move_bits(engine, dst, src)
+
+        def turn_scales(b, number):
+            bank["ts", b] = new_bank(number)
             for j in range(4):
-                nc.tensor.transpose(bank["ts", b][:, 2 * j : 2 * j + P], tsg[b][:].rearrange("p (s j) -> p j s", j=4)[:, j, :], ident[:])
+                src = dealt[b][:] if b else tsg[b][:].rearrange("p (s j) -> p j s", j=4)
+                nc.tensor.transpose(bank["ts", b][:, chunk(j)], src[:, j, :], ident[:])
 
-        def copy(engine, dst, src):
-            if engine is nc.scalar:
-                nc.scalar.activation(out=dst, in_=src, func=COPY)
-            else:
-                nc.vector.tensor_copy(out=dst, in_=src)
+        def deal_scales():
+            dealt[1] = new([P, 4, P], F32, "dealt", tag="scale_tab")
+            nc.vector.tensor_copy(out=dealt[1][:], in_=tsg[1][:].rearrange("p (s j) -> p j s", j=4))
 
         def scale_columns(engine, b):
-            copy(engine, ts_col[b][:], bank["ts", b][:, 0:8].rearrange("p (k e) -> p k e", e=2)[:, :, 0])
+            move(engine, ts_col[b][:], bank["ts", b][:].rearrange("s (j r) -> s j r", j=4)[:, :, P - B + b])
 
-        def spread_scales(b):
-            bank["tsb", b] = new_bank((5, 3)[b])
+        def spread_scales(b, number):
+            bank["tsb", b] = new_bank(number)
             for j in range(4):
                 nc.tensor.transpose(bank["tsb", b][:, chunk(j)], ts_col[b][:, j : j + 1].to_broadcast([P, P]), ident[:])
 
         def scale_rows(engine, b):
-            copy(engine, ts_rows[b][:].rearrange("q j s -> q (j s)"), bank["tsb", b][:])
+            move(engine, ts_rows[b][:].rearrange("q j s -> q (j s)"), bank["tsb", b][:])
 
-        def cast_queries(b):
-            if b == 0:
-                nc.gpsimd.tensor_scalar(q_bf[b][:], q_raw[b][:].rearrange("p t q -> p q t"), 1.0, 0.0, MULT, ADD)
-            else:
-                dst = q_bf[b][:].rearrange("p (c i) t -> p c t i", i=4)
-                nc.scalar.activation(out=dst, in_=q_raw[b][:].rearrange("p t (c i) -> p c t i", i=4), func=COPY)
+        def cast_queries(engine, b):
+            move(engine, q_bf[b][:].rearrange("p (c i) t -> p c t i", i=4), q_raw[b][:].rearrange("p t (c i) -> p c t i", i=4))
 
         def quantise(codes, scales, src):
             nc.vector.quantize_mx(out=codes.bitcast(FP8X4), scales=scales, in_=src)
@@ -179,29 +175,32 @@ def tile_attend_x_mla_gate_seg_kernel(tc, qT, cT, ts, ch, og, offs, out):
         def quantise_keys(b, cols):
             quantise(k_codes[b][:, cols], k_scales[b][:, cols], kb[b][:, 4 * cols.start : 4 * cols.stop])
 
-        def quantise_values(b, cols=ALL):
-            quantise(v_codes[b][:, cols], v_scales[b][:, cols], vb[b, cols.start // 256][:] if b == 0 else vb[b][:])
+        def value_scales(b, cols):
+            return v_scales[b][:, cols] if b else v_scales[b, cols.start // 256][:]
+
+        def quantise_values(b, cols):
+            quantise(v_codes[b][:, cols], value_scales(b, cols), vb[b][:] if b else vb[b, cols.start // 256][:])
 
         def quantise_weights(b, rows=slice(0, NQ)):
             quantise(w_codes[b][:, rows], w_scales[b][:, rows], wb[b][:, rows].rearrange("p n t -> p (n t)"))
 
-        def scores(b, cols, number):
-            tile = new_bank(number, cols.stop - cols.start)
-            bank["score", b, cols.start] = tile
+        def multiply(dst, stationary, moving):
             nc.tensor.matmul_mx(
-                out=tile[:],
-                lhsT=q_codes[b][:].bitcast(FP8X4),
-                lhsT_scale=q_scales[b][:],
-                rhs=k_codes[b][:, cols].bitcast(FP8X4),
-                rhs_scale=k_scales[b][:, cols],
+                out=dst,
+                lhsT=stationary[0].bitcast(FP8X4),
+                lhsT_scale=stationary[1],
+                rhs=moving[0].bitcast(FP8X4),
+                rhs_scale=moving[1],
                 start=True,
                 stop=True,
             )
 
-        def scale_scores(b, cols):
+        def scores(b, cols, place):
+            multiply(place, (q_codes[b][:], q_scales[b][:]), (k_codes[b][:, cols], k_scales[b][:, cols]))
+
+        def scale_scores(b, cols, place):
             rows = slice(cols.start // 4, cols.stop // 4)
-            src = bank["score", b, cols.start][:].rearrange("q (s j) -> q j s", j=4)
-            nc.vector.tensor_tensor(a_t[b][:, :, rows], src, ts_rows[b][:, :, rows], MULT)
+            nc.vector.tensor_tensor(a_t[b][:, :, rows], place.rearrange("q (s j) -> q j s", j=4), ts_rows[b][:, :, rows], MULT)
 
         def maximum(b):
             nc.vector.tensor_reduce(out=neg_m[b][:], in_=a_t[b][:].rearrange("q j s -> q (j s)"), axis=AXIS_X, op=MAX, negate=True)
@@ -209,31 +208,40 @@ def tile_attend_x_mla_gate_seg_kernel(tc, qT, cT, ts, ch, og, offs, out):
         def exponentials(b, js, total):
             nc.scalar.activation(out=p[b][:, js], in_=a_t[b][:, js], func=EXP, bias=neg_m[b][:], accum_out=total)
 
-        def add_sums():
-            nc.vector.tensor_reduce(out=l_sum[:, 1:2], in_=l_part[:], axis=AXIS_X, op=ADD)
+        def double_first_sum():
+            nc.scalar.activation(out=l_twice[:, 0:1], in_=l_first[:], func=COPY, scale=2.0)
+
+        def double_second_sum():
+            nc.vector.tensor_scalar(l_twice[:, 1:2], l_part[:, 0:1], l_part[:, 1:2], 2.0, ADD, MULT)
 
         def invert_sums():
-            nc.vector.reciprocal(inv_l[:], l_sum[:])
+            nc.vector.reciprocal(inv_l[:], l_twice[:])
 
-        def turn_values(b, t):
-            u = t // 2
-            if t % 2 == 0:
-                bank["v", b, u] = new_bank((3, 4, 2, 4)[2 * b + u])
+        def turn_values(b, t, place):
             words = planes[b][:, t * N : (t + 1) * N].bitcast(F32).rearrange("p (s h) -> p h s", h=2)
             for h in range(2):
-                nc.tensor.transpose(bank["v", b, u][:, chunk(2 * (t % 2) + h)], words[:, h, :], ident[:])
+                nc.tensor.transpose(place[:, chunk(h)], words[:, h, :], ident[:])
 
-        def copy_values(b, u):
-            if b == 0:
-                dst = vb[b, u][:].bitcast(F32).rearrange("s (t p h) -> s t p h", t=2, h=2)
-                nc.scalar.copy(out=dst, in_=bank["v", b, u][:].rearrange("s (t h p) -> s t p h", t=2, h=2))
-            else:
-                dst = vb[b][:].bitcast(F32).rearrange("s (p u w) -> s u p w", u=2, w=4)[:, u]
-                nc.scalar.copy(out=dst, in_=bank["v", b, u][:].rearrange("s (w p) -> s p w", w=4))
+        def turn_first_values(t, number):
+            bank["v", 0, t] = new_bank(number, 2 * P)
+            turn_values(0, t, bank["v", 0, t])
 
-        def turn_weights(b, js):
+        def copy_first_values(engine, t):
+            dst = vb[0, t // 2][:].bitcast(F32)[:, chunk(2 * (t % 2), 2)].rearrange("s (p h) -> s p h", h=2)
+            move_bits(engine, dst, bank["v", 0, t][:].rearrange("s (h p) -> s p h", h=2))
+
+        def turn_second_values(u, number):
+            bank["v", 1, u] = new_bank(number)
+            for t in range(2):
+                turn_values(1, 2 * u + t, bank["v", 1, u][:, chunk(2 * t, 2)])
+
+        def copy_second_values(u):
+            dst = vb[1][:].bitcast(F32).rearrange("s (p u w) -> s u p w", u=2, w=4)[:, u]
+            nc.scalar.copy(out=dst, in_=bank["v", 1, u][:].rearrange("s (w p) -> s p w", w=4))
+
+        def turn_weights(b, js, number=None):
             if js.start == 0:
-                bank["w", b] = new_bank((6, 7)[b])
+                bank["w", b] = new_bank(number)
             for j in range(js.start, js.stop):
                 nc.tensor.transpose(bank["w", b][:, chunk(j)], p[b][:, j, :], ident[:])
 
@@ -246,156 +254,134 @@ def tile_attend_x_mla_gate_seg_kernel(tc, qT, cT, ts, ch, og, offs, out):
                 MULT,
             )
 
-        def products(b, cols, number):
-            tile = new_bank(number, cols.stop - cols.start)
-            bank["y", b, cols.start] = tile
-            nc.tensor.matmul_mx(
-                out=tile[:],
-                lhsT=w_codes[b][:].bitcast(FP8X4),
-                lhsT_scale=w_scales[b][:],
-                rhs=v_codes[b][:, cols].bitcast(FP8X4),
-                rhs_scale=v_scales[b][:, cols],
-                start=True,
-                stop=True,
-            )
+        def products(b, cols, place):
+            multiply(place, (w_codes[b][:], w_scales[b][:]), (v_codes[b][:, cols], value_scales(b, cols)))
 
         def gate_tanh(b):
             nc.scalar.activation(out=th[b][:], in_=og_sb[b][:], func=TANH, scale=0.5)
 
         def gate_channels(b):
-            nc.vector.scalar_tensor_tensor(
-                out=gate[b][:].rearrange("q (p t) -> q p t", t=4),
-                in0=th[b][:].rearrange("q (p t) -> q p t", t=4),
-                scalar=1.0,
-                in1=bank["ch"][:].rearrange("q (t p) -> q p t", t=4),
-                op0=ADD,
-                op1=MULT,
-            )
+            nc.vector.scalar_tensor_tensor(out=gate[b][:], in0=th[b][:], scalar=1.0, in1=ch_sb[:], op0=ADD, op1=MULT)
 
-        def finish(b, cols):
-            y, dst, factor = bank["y", b, cols.start][:], o[b][:, cols], gate[b][:, cols]
+        def finish(b, cols, y):
+            dst, factor = o[b][:, cols], gate[b][:, cols]
             if b == 0:
-                y = y.rearrange("q (t p) -> q p t", t=4)
+                y = y.rearrange("q (t p) -> q p t", t=4)[:, cols.start // 4 : cols.stop // 4]
                 dst, factor = dst.rearrange("q (p t) -> q p t", t=4), factor.rearrange("q (p t) -> q p t", t=4)
             nc.vector.scalar_tensor_tensor(out=dst, in0=y, scalar=inv_l[:, b : b + 1], in1=factor, op0=MULT, op1=MULT)
             nc.sync.dma_start(out=out[b][:, cols], in_=o[b][:, cols])
 
-        load_plane(0, 0)
         nc.sync.dma_start(offsets[:], offs)
-        load_channels()
-        load_scales(0)
-        load_plane(0, 1)
-        load_scales(1)
-        load_plane(0, 2)
+        load_scales()
+        for t in range(4):
+            load_plane(0, t)
         load_queries(0)
-        load_plane(0, 3)
         for t in range(4):
             load_plane(1, t)
         load_queries(1)
         load_gate(0)
+        load_channels()
         load_gate(1)
+        preload_exp()
+        clear_scales()
         nc.vector.memset(ident[:], 0.0)
         make_identity(nc, ident[:], nomemset=True)
-        preload_exp()
-        spread_channels()
-        gather_scales(0)
+        gather_scales(nc.vector, 0)
+        gather_scales(nc.scalar, 1)
         gather_plane(nc.scalar, 0, 0)
-        gather_scales(1)
-        gather_plane(nc.scalar, 0, 1)
-        turn_values(0, 0)
-        turn_scales(0)
-        turn_values(0, 1)
-        gather_plane(nc.scalar, 0, 2, LEFT)
-        gather_plane(nc.vector, 0, 2, RIGHT)
-        cast_queries(0)
-        ts_col[0] = new([P, 4], F32, "ts_col0", tag="win01")
-        scale_columns(nc.vector, 0)
-        vb[0, 0] = new([P, 2 * D], BF16, "vb00", tag="win02")
-        copy_values(0, 0)
-        spread_scales(0)
-        turn_values(0, 2)
-        turn_scales(1)
-        quantise_queries(0)
-        ts_rows[0] = new([P, 4, P], F32, "ts_rows0")
-        scale_rows(nc.vector, 0)
-        for c in range(4):
-            gather_plane(nc.scalar, 0, 3, chunk(c))
-        turn_values(0, 3)
-        for c in range(3):
-            weave(0, chunk(c))
-        quantise_keys(0, LEFT)
-        weave(0, chunk(3))
-        quantise_values(0, LEFT)
-        quantise_keys(0, RIGHT)
-        gather_plane(nc.scalar, 1, 0)
-        middle = new([P, D + 16], F32, "middle", tag="win10")
-        vb[0, 1] = middle[:, 0:D].bitcast(BF16)
-        ts_col[1] = middle[:, D : D + 4]
-        copy_values(0, 1)
+        deal_scales()
+        turn_scales(0, 0)
+        turn_scales(1, 5)
+        scale_columns(nc.scalar, 0)
         scale_columns(nc.scalar, 1)
-        gather_plane(nc.scalar, 1, 1)
-        scores(0, LEFT, 3)
-        scores(0, RIGHT, 2)
-        scale_scores(0, LEFT)
-        gather_plane(nc.vector, 1, 2, slice(SHARE, N))
-        scale_scores(0, RIGHT)
-        turn_values(1, 0)
-        turn_values(1, 1)
-        spread_scales(1)
-        gather_plane(nc.scalar, 1, 2, slice(0, SHARE))
+        gather_plane(nc.vector, 0, 1)
+        turn_first_values(0, 0)
+        spread_scales(0, 1)
+        gather_plane(nc.scalar, 0, 2)
+        turn_first_values(1, 3)
+        spread_scales(1, 6)
+        vb[0, 0] = new([P, 2 * D], BF16, "vb00")
+        copy_first_values(nc.vector, 0)
+        ts_rows[0] = new([P, 4, P], F32, "ts_rows0", tag="win01")
+        scale_rows(nc.vector, 0)
+        copy_first_values(nc.vector, 1)
+        gather_plane(nc.vector, 0, 3, slice(LAST_SHARE, N))
+        gather_plane(nc.scalar, 0, 3, slice(0, LAST_SHARE))
+        turn_first_values(2, 2)
+        turn_first_values(3, 4)
+        cast_queries(nc.scalar, 0)
+        weave(nc.vector, 0, RIGHT)
+        weave(nc.vector, 0, LEFT)
+        vb[0, 1] = new([P, 2 * D], BF16, "vb01", tag="win03")
+        copy_first_values(nc.scalar, 2)
+        copy_first_values(nc.scalar, 3)
+        quantise_keys(0, RIGHT)
+        quantise_queries(0)
+        quantise_keys(0, LEFT)
+        gather_plane(nc.scalar, 1, 0)
+        first_scores = new_bank(0)
+        scores(0, RIGHT, first_scores[:, RIGHT])
+        scores(0, LEFT, first_scores[:, LEFT])
+        quantise_values(0, LEFT)
+        gather_plane(nc.scalar, 1, 1, slice(0, SHARE))
+        gather_plane(nc.vector, 1, 1, slice(SHARE, N))
+        scale_scores(0, ALL, first_scores[:])
+        gather_plane(nc.scalar, 1, 2)
+        v_scales[0, 1] = new([P, D // 2], U8, "v_scales01", tag="win11")
         quantise_values(0, RIGHT)
         neg_m[0] = new([P, 1], F32, "neg_m0")
         maximum(0)
+        turn_second_values(0, 0)
         for c in range(4):
             gather_plane(nc.scalar, 1, 3, chunk(c))
-        turn_values(1, 2)
-        turn_values(1, 3)
-        cast_queries(1)
-        for c in range(3):
-            weave(1, chunk(c))
-        quantise_keys(1, LEFT)
-        weave(1, chunk(3))
-        quantise_queries(1)
-        quantise_keys(1, RIGHT)
-        gate_tanh(0)
-        ts_rows[1] = lay([P, 4, P], F32, "ts_rows1", 0)
-        scale_rows(nc.scalar, 1)
-        late = new([P, N + 2 * D], F32, "late", tag="og_sb0")
+        cast_queries(nc.scalar, 1)
+        late = lay([P, N + 2 * D], F32, "late", 0)
         p[0] = late[:, 0:N].rearrange("q (j s) -> q j s", j=4)
         vb[1] = late[:, N : N + 2 * D].bitcast(BF16)
-        exponentials(0, slice(0, 4), l_sum[:, 0:1])
-        copy_values(1, 0)
-        copy_values(1, 1)
+        ts_rows[1] = lay([P, 4, P], F32, "ts_rows1", 8064)
+        for c in range(4):
+            weave(nc.vector, 1, chunk(c))
+        quantise_keys(1, LEFT)
+        quantise_queries(1)
+        quantise_keys(1, RIGHT)
+        turn_second_values(1, 3)
+        left_scores, right_scores = new_bank(2, N // 2), new_bank(4, N // 2)
+        scores(1, LEFT, left_scores[:])
+        scores(1, RIGHT, right_scores[:])
+        gate_tanh(0)
+        scale_rows(nc.scalar, 1)
+        exponentials(0, slice(0, 4), l_first[:])
+        copy_second_values(0)
+        copy_second_values(1)
+        double_first_sum()
         gate_tanh(1)
-        gate[0] = new([P, D], F32, "gate0", tag="planes1")
         gate_channels(0)
-        scores(1, LEFT, 6)
-        scores(1, RIGHT, 1)
-        scale_scores(1, LEFT)
-        turn_weights(0, slice(0, 4))
-        scale_scores(1, RIGHT)
+        scale_scores(1, LEFT, left_scores[:])
+        scale_scores(1, RIGHT, right_scores[:])
+        turn_weights(0, slice(0, 4), 4)
         maximum(1)
-        wb[0] = lay([P, NQ, 4], BF16, "wb0", 0)
-        v_scales[1] = lay([P, D], U8, "v_scales1", 1024)
-        gate[1] = lay([P, D], F32, "gate1", 1536)
+        v_scales[1] = lay([P, D], U8, "v_scales1", 8128)
+        gate[1] = lay([P, D], F32, "gate1", 8640)
+        quantise_values(1, ALL)
         scale_weights(0)
-        quantise_values(1)
-        quantise_weights(0)
         gate_channels(1)
-        for h in range(2):
-            js = slice(2 * h, 2 * h + 2)
-            exponentials(1, js, l_part[:, h : h + 1])
-            turn_weights(1, js)
-        products(0, ALL, 5)
-        add_sums()
+        quantise_weights(0)
+        for js in (LOW, HIGH):
+            exponentials(1, js, l_part[:, js.start // 2 : js.stop // 2])
+            turn_weights(1, js, 6)
+        first_products = new_bank(7)
+        products(0, LEFT, first_products[:, LEFT])
+        products(0, RIGHT, first_products[:, RIGHT])
+        double_second_sum()
         scale_weights(1, slice(0, 64))
-        invert_sums()
         scale_weights(1, slice(64, NQ))
         quantise_weights(1, slice(0, 64))
+        invert_sums()
         quantise_weights(1, slice(64, NQ))
-        o[0] = new([P, D], F32, "o0", tag="win10")
-        finish(0, ALL)
-        products(1, LEFT, 3)
-        products(1, RIGHT, 1)
-        finish(1, LEFT)
-        finish(1, RIGHT)
+        left_products, right_products = new_bank(0, N // 2), new_bank(1, N // 2)
+        products(1, LEFT, left_products[:])
+        products(1, RIGHT, right_products[:])
+        finish(0, LEFT, first_products[:])
+        finish(0, RIGHT, first_products[:])
+        finish(1, LEFT, left_products[:])
+        finish(1, RIGHT, right_products[:])

@@ -1,7 +1,6 @@
 from contextlib import ExitStack
 
 import concourse.mybir as mybir
-from concourse.masks import make_identity
 
 FLOPS = 2 * 2 * 2 * 128 * 512 * 512
 
@@ -14,6 +13,7 @@ U8 = mybir.dt.uint8
 FP8X4 = mybir.dt.float8_e4m3fn_x4
 MULT = mybir.AluOpType.mult
 ADD = mybir.AluOpType.add
+EQUAL = mybir.AluOpType.is_equal
 MAX = mybir.AluOpType.max
 COPY = mybir.ActivationFunctionType.Copy
 EXP = mybir.ActivationFunctionType.Exp
@@ -30,8 +30,7 @@ NQ = 128
 LIST = N // 16
 ALL, LEFT, RIGHT = slice(0, N), slice(0, N // 2), slice(N // 2, N)
 LOW, HIGH = slice(0, 2), slice(2, 4)
-SHARE = 288
-LAST_SHARE = 320
+SHARE = 384
 
 
 def chunk(c, n=1):
@@ -71,7 +70,7 @@ def tile_attend_x_mla_gate_seg_kernel(tc, qT, cT, ts, ch, og, offs, out):
         q_bf = each([P, NQ, 4], BF16, "q_bf")
         q_codes, q_scales = each([P, NQ], U32, "q_codes"), each([P, NQ], U8, "q_scales")
         tsg = each([P, N], F32, "tsg")
-        ts_col = each([P, 4], F32, "ts_col")
+        ts_col = {0: new([P, 4], F32, "ts_col0")}
         ts_rows = {}
         neg_m, p, vb = {}, {}, {}
         a_t = each([P, 4, P], F32, "a_t")
@@ -86,7 +85,6 @@ def tile_attend_x_mla_gate_seg_kernel(tc, qT, cT, ts, ch, og, offs, out):
         w_codes, w_scales = each([P, NQ], U32, "w_codes"), each([P, NQ], U8, "w_scales")
         th, o = each([P, D], F32, "th"), each([P, D], F32, "o")
         gate = {0: new([P, D], F32, "gate0")}
-        dealt = {}
         bank = {}
 
         ident = new([P, P], F32, "ident")
@@ -96,6 +94,16 @@ def tile_attend_x_mla_gate_seg_kernel(tc, qT, cT, ts, ch, og, offs, out):
         def preload_exp():
             nc.vector.memset(warm[:], 0.0)
             nc.scalar.activation(out=warmed[:], in_=warm[:], func=EXP)
+
+        def build_identity():
+            ones, ramp, turned = (new([P, 32], F32, name) for name in ("ones", "ramp", "turned"))
+            nc.vector.memset(ones[:], 1.0)
+            nc.vector.tensor_tensor_scan(ramp[:], ones[:], ones[:], -1.0, MULT, ADD)
+            nc.vector.transpose(turned[:], ramp[:])
+            nc.vector.memset(ident[:], 0.0)
+            for first in range(0, P, 32):
+                rows = slice(first, first + 32)
+                nc.vector.tensor_tensor(ident[rows, rows], ramp[rows, :], turned[rows, :], EQUAL)
 
         def load_plane(b, t):
             cols = slice(b * SEG, (b + 1) * SEG)
@@ -145,12 +153,7 @@ def tile_attend_x_mla_gate_seg_kernel(tc, qT, cT, ts, ch, og, offs, out):
         def turn_scales(b, number):
             bank["ts", b] = new_bank(number)
             for j in range(4):
-                src = dealt[b][:] if b else tsg[b][:].rearrange("p (s j) -> p j s", j=4)
-                nc.tensor.transpose(bank["ts", b][:, chunk(j)], src[:, j, :], ident[:])
-
-        def deal_scales():
-            dealt[1] = new([P, 4, P], F32, "dealt", tag="scale_tab")
-            nc.vector.tensor_copy(out=dealt[1][:], in_=tsg[1][:].rearrange("p (s j) -> p j s", j=4))
+                nc.tensor.transpose(bank["ts", b][:, chunk(j)], tsg[b][:].rearrange("p (s j) -> p j s", j=4)[:, j, :], ident[:])
 
         def scale_columns(engine, b):
             move(engine, ts_col[b][:], bank["ts", b][:].rearrange("s (j r) -> s j r", j=4)[:, :, P - B + b])
@@ -230,6 +233,15 @@ def tile_attend_x_mla_gate_seg_kernel(tc, qT, cT, ts, ch, og, offs, out):
             dst = vb[0, t // 2][:].bitcast(F32)[:, chunk(2 * (t % 2), 2)].rearrange("s (p h) -> s p h", h=2)
             move_bits(engine, dst, bank["v", 0, t][:].rearrange("s (h p) -> s p h", h=2))
 
+        def turn_last_values(number):
+            bank["v", 0, 2] = new_bank(number)
+            for t in range(2):
+                turn_values(0, 2 + t, bank["v", 0, 2][:, chunk(2 * t, 2)])
+
+        def copy_last_values():
+            dst = vb[0, 1][:].bitcast(F32).rearrange("s (t p h) -> s t p h", t=2, h=2)
+            nc.vector.tensor_copy(out=dst, in_=bank["v", 0, 2][:].rearrange("s (t h p) -> s t p h", t=2, h=2))
+
         def turn_second_values(u, number):
             bank["v", 1, u] = new_bank(number)
             for t in range(2):
@@ -283,46 +295,44 @@ def tile_attend_x_mla_gate_seg_kernel(tc, qT, cT, ts, ch, og, offs, out):
         load_channels()
         load_gate(1)
         preload_exp()
+        build_identity()
         clear_scales()
-        nc.vector.memset(ident[:], 0.0)
-        make_identity(nc, ident[:], nomemset=True)
         gather_scales(nc.vector, 0)
         gather_scales(nc.scalar, 1)
         gather_plane(nc.scalar, 0, 0)
-        deal_scales()
         turn_scales(0, 0)
-        turn_scales(1, 5)
         scale_columns(nc.scalar, 0)
-        scale_columns(nc.scalar, 1)
         gather_plane(nc.vector, 0, 1)
         turn_first_values(0, 0)
         spread_scales(0, 1)
         gather_plane(nc.scalar, 0, 2)
         turn_first_values(1, 3)
-        spread_scales(1, 6)
-        vb[0, 0] = new([P, 2 * D], BF16, "vb00")
+        early = new([P, D + N], F32, "early", tag="win01")
+        vb[0, 0] = early[:, 0:D].bitcast(BF16)
+        ts_rows[0] = early[:, D : D + N].rearrange("q (j s) -> q j s", j=4)
         copy_first_values(nc.vector, 0)
-        ts_rows[0] = new([P, 4, P], F32, "ts_rows0", tag="win01")
         scale_rows(nc.vector, 0)
         copy_first_values(nc.vector, 1)
-        gather_plane(nc.vector, 0, 3, slice(LAST_SHARE, N))
-        gather_plane(nc.scalar, 0, 3, slice(0, LAST_SHARE))
-        turn_first_values(2, 2)
-        turn_first_values(3, 4)
-        cast_queries(nc.scalar, 0)
-        weave(nc.vector, 0, RIGHT)
+        gather_plane(nc.scalar, 0, 3, LEFT)
+        gather_plane(nc.scalar, 0, 3, RIGHT)
+        turn_last_values(4)
+        turn_scales(1, 1)
+        cast_queries(nc.vector, 0)
         weave(nc.vector, 0, LEFT)
+        weave(nc.vector, 0, RIGHT)
         vb[0, 1] = new([P, 2 * D], BF16, "vb01", tag="win03")
-        copy_first_values(nc.scalar, 2)
-        copy_first_values(nc.scalar, 3)
-        quantise_keys(0, RIGHT)
-        quantise_queries(0)
         quantise_keys(0, LEFT)
+        quantise_queries(0)
+        quantise_keys(0, RIGHT)
         gather_plane(nc.scalar, 1, 0)
         first_scores = new_bank(0)
-        scores(0, RIGHT, first_scores[:, RIGHT])
         scores(0, LEFT, first_scores[:, LEFT])
+        scores(0, RIGHT, first_scores[:, RIGHT])
         quantise_values(0, LEFT)
+        copy_last_values()
+        ts_col[1] = new([P, 4], F32, "ts_col1", tag="kb0")
+        scale_columns(nc.vector, 1)
+        spread_scales(1, 6)
         gather_plane(nc.scalar, 1, 1, slice(0, SHARE))
         gather_plane(nc.vector, 1, 1, slice(SHARE, N))
         scale_scores(0, ALL, first_scores[:])
@@ -344,8 +354,8 @@ def tile_attend_x_mla_gate_seg_kernel(tc, qT, cT, ts, ch, og, offs, out):
         quantise_keys(1, LEFT)
         quantise_queries(1)
         quantise_keys(1, RIGHT)
-        turn_second_values(1, 3)
-        left_scores, right_scores = new_bank(2, N // 2), new_bank(4, N // 2)
+        turn_second_values(1, 1)
+        left_scores, right_scores = new_bank(2, N // 2), new_bank(3, N // 2)
         scores(1, LEFT, left_scores[:])
         scores(1, RIGHT, right_scores[:])
         gate_tanh(0)
@@ -358,7 +368,7 @@ def tile_attend_x_mla_gate_seg_kernel(tc, qT, cT, ts, ch, og, offs, out):
         gate_channels(0)
         scale_scores(1, LEFT, left_scores[:])
         scale_scores(1, RIGHT, right_scores[:])
-        turn_weights(0, slice(0, 4), 4)
+        turn_weights(0, slice(0, 4), 3)
         maximum(1)
         v_scales[1] = lay([P, D], U8, "v_scales1", 8128)
         gate[1] = lay([P, D], F32, "gate1", 8640)
@@ -378,7 +388,7 @@ def tile_attend_x_mla_gate_seg_kernel(tc, qT, cT, ts, ch, og, offs, out):
         quantise_weights(1, slice(0, 64))
         invert_sums()
         quantise_weights(1, slice(64, NQ))
-        left_products, right_products = new_bank(0, N // 2), new_bank(1, N // 2)
+        left_products, right_products = new_bank(0, N // 2), new_bank(4, N // 2)
         products(1, LEFT, left_products[:])
         products(1, RIGHT, right_products[:])
         finish(0, LEFT, first_products[:])

@@ -30,7 +30,7 @@ NQ = 128
 LIST = N // 16
 ALL, LEFT, RIGHT = slice(0, N), slice(0, N // 2), slice(N // 2, N)
 LOW, HIGH = slice(0, 2), slice(2, 4)
-SHARE = 384
+SHARE = 288
 
 
 def chunk(c, n=1):
@@ -80,7 +80,7 @@ def tile_attend_x_mla_gate_seg_kernel(tc, qT, cT, ts, ch, og, offs, out):
         l_part = new([P, 2], F32, "l_part")
         l_twice = new([P, B], F32, "l_twice")
         inv_l = new([P, B], F32, "inv_l")
-        v_codes, v_scales = each([P, D], U32, "v_codes"), {(0, 0): new([P, D // 2], U8, "v_scales00")}
+        v_codes, v_scales = each([P, D], U32, "v_codes"), {}
         wb = each([P, NQ, 4], BF16, "wb")
         w_codes, w_scales = each([P, NQ], U32, "w_codes"), each([P, NQ], U8, "w_scales")
         th, o = each([P, D], F32, "th"), each([P, D], F32, "o")
@@ -328,6 +328,7 @@ def tile_attend_x_mla_gate_seg_kernel(tc, qT, cT, ts, ch, og, offs, out):
         first_scores = new_bank(0)
         scores(0, LEFT, first_scores[:, LEFT])
         scores(0, RIGHT, first_scores[:, RIGHT])
+        v_scales[0, 0] = new([P, D // 2], U8, "v_scales00", tag="q_raw0")
         quantise_values(0, LEFT)
         copy_last_values()
         ts_col[1] = new([P, 4], F32, "ts_col1", tag="kb0")

@@ -84,7 +84,7 @@ def tile_attend_x_mla_gate_seg_kernel(tc, qT, cT, ts, ch, og, offs, out):
         wb = each([P, NQ, 4], BF16, "wb")
         w_codes, w_scales = each([P, NQ], U32, "w_codes"), each([P, NQ], U8, "w_scales")
         th, o = each([P, D], F32, "th"), each([P, D], F32, "o")
-        gate = {0: new([P, D], F32, "gate0")}
+        gate = {(0, 0): new([P, D], F32, "gate0"), (1, 0): new([P, D // 2], F32, "gate10")}
         bank = {}
 
         ident = new([P, P], F32, "ident")
@@ -272,11 +272,11 @@ def tile_attend_x_mla_gate_seg_kernel(tc, qT, cT, ts, ch, og, offs, out):
         def gate_tanh(b):
             nc.scalar.activation(out=th[b][:], in_=og_sb[b][:], func=TANH, scale=0.5)
 
-        def gate_channels(b):
-            nc.vector.scalar_tensor_tensor(out=gate[b][:], in0=th[b][:], scalar=1.0, in1=ch_sb[:], op0=ADD, op1=MULT)
+        def gate_channels(b, cols):
+            nc.vector.scalar_tensor_tensor(out=gate[b, cols.start][:], in0=th[b][:, cols], scalar=1.0, in1=ch_sb[:, cols], op0=ADD, op1=MULT)
 
         def finish(b, cols, y):
-            dst, factor = o[b][:, cols], gate[b][:, cols]
+            dst, factor = o[b][:, cols], gate[b, cols.start][:] if b else gate[b, 0][:, cols]
             if b == 0:
                 y = y.rearrange("q (t p) -> q p t", t=4)[:, cols.start // 4 : cols.stop // 4]
                 dst, factor = dst.rearrange("q (p t) -> q p t", t=4), factor.rearrange("q (p t) -> q p t", t=4)
@@ -292,8 +292,8 @@ def tile_attend_x_mla_gate_seg_kernel(tc, qT, cT, ts, ch, og, offs, out):
             load_plane(1, t)
         load_queries(1)
         load_gate(0)
-        load_channels()
         load_gate(1)
+        load_channels()
         preload_exp()
         build_identity()
         clear_scales()
@@ -361,21 +361,22 @@ def tile_attend_x_mla_gate_seg_kernel(tc, qT, cT, ts, ch, og, offs, out):
         scores(1, RIGHT, right_scores[:])
         gate_tanh(0)
         scale_rows(nc.scalar, 1)
+        gate_tanh(1)
         exponentials(0, slice(0, 4), l_first[:])
         copy_second_values(0)
         copy_second_values(1)
         double_first_sum()
-        gate_tanh(1)
-        gate_channels(0)
+        gate_channels(0, ALL)
         scale_scores(1, LEFT, left_scores[:])
         scale_scores(1, RIGHT, right_scores[:])
         turn_weights(0, slice(0, 4), 3)
+        gate_channels(1, LEFT)
         maximum(1)
         v_scales[1] = lay([P, D], U8, "v_scales1", 8128)
-        gate[1] = lay([P, D], F32, "gate1", 8640)
-        quantise_values(1, ALL)
+        gate[1, RIGHT.start] = lay([P, D // 2], F32, "gate11", 8640)
+        gate_channels(1, RIGHT)
         scale_weights(0)
-        gate_channels(1)
+        quantise_values(1, ALL)
         quantise_weights(0)
         for js in (LOW, HIGH):
             exponentials(1, js, l_part[:, js.start // 2 : js.stop // 2])

@@ -59,9 +59,10 @@ def tile_attend_x_mla_gate_seg_kernel(tc, qT, cT, ts, ch, og, offs, out):
         def new_bank(number, columns=N):
             return psum.tile([P, columns], F32, name="bank", tag=f"bank{number}")
 
-        win = {(b, t): new([P, (b + 1) * SEG], F32, f"win{b}{t}") for b in range(B) for t in range(4)}
+        win = {(b, t): new([P, (b + 1) * SEG], F32, f"win{b}{t}") for b in range(B) for t in range(4 - b)}
+        win[1, 3] = lay([P, T], F32, "win13", 6080)
         scale_tab = new([P, T], F32, "scale_tab")
-        q_raw = [new([P, 4, NQ], F32, "q_raw0"), lay([P, 4, NQ], F32, "q_raw1", 6080)]
+        q_raw = each([P, 4, NQ], F32, "q_raw")
         ch_sb = new([P, D], F32, "ch_sb")
         og_sb = each([P, D], F32, "og_sb")
         planes = each([P, 4 * N], BF16, "planes")
@@ -345,15 +346,17 @@ def tile_attend_x_mla_gate_seg_kernel(tc, qT, cT, ts, ch, og, offs, out):
         turn_second_values(0, 0)
         for c in range(4):
             gather_plane(nc.scalar, 1, 3, chunk(c))
-        cast_queries(nc.scalar, 1)
+        weave(nc.vector, 1, chunk(0))
+        weave(nc.vector, 1, chunk(1))
+        cast_queries(nc.vector, 1)
+        weave(nc.vector, 1, chunk(2))
+        weave(nc.vector, 1, chunk(3))
         late = lay([P, N + 2 * D], F32, "late", 0)
         p[0] = late[:, 0:N].rearrange("q (j s) -> q j s", j=4)
         vb[1] = late[:, N : N + 2 * D].bitcast(BF16)
-        ts_rows[1] = lay([P, 4, P], F32, "ts_rows1", 8064)
-        for c in range(4):
-            weave(nc.vector, 1, chunk(c))
-        quantise_keys(1, LEFT)
+        ts_rows[1] = lay([P, 4, P], F32, "ts_rows1", 14208)
         quantise_queries(1)
+        quantise_keys(1, LEFT)
         quantise_keys(1, RIGHT)
         turn_second_values(1, 1)
         left_scores, right_scores = new_bank(2, N // 2), new_bank(3, N // 2)
@@ -372,8 +375,8 @@ def tile_attend_x_mla_gate_seg_kernel(tc, qT, cT, ts, ch, og, offs, out):
         turn_weights(0, slice(0, 4), 3)
         gate_channels(1, LEFT)
         maximum(1)
-        v_scales[1] = lay([P, D], U8, "v_scales1", 8128)
-        gate[1, RIGHT.start] = lay([P, D // 2], F32, "gate11", 8640)
+        v_scales[1] = lay([P, D], U8, "v_scales1", 14272)
+        gate[1, RIGHT.start] = lay([P, D // 2], F32, "gate11", 14784)
         gate_channels(1, RIGHT)
         scale_weights(0)
         quantise_values(1, ALL)

from contextlib import ExitStack

import concourse.mybir as mybir

FLOPS = 2 * 2 * 2 * 128 * 512 * 512

F32 = mybir.dt.float32
BF16 = mybir.dt.bfloat16
U32 = mybir.dt.uint32
I32 = mybir.dt.int32
U16 = mybir.dt.uint16
U8 = mybir.dt.uint8
FP8X4 = mybir.dt.float8_e4m3fn_x4
MULT = mybir.AluOpType.mult
ADD = mybir.AluOpType.add
EQUAL = mybir.AluOpType.is_equal
MAX = mybir.AluOpType.max
COPY = mybir.ActivationFunctionType.Copy
EXP = mybir.ActivationFunctionType.Exp
TANH = mybir.ActivationFunctionType.Tanh
AXIS_X = mybir.AxisListType.X

P = 128
B = 2
N = 512
T = 2048
SEG = T // B
D = 512
NQ = 128
LIST = N // 16
ALL, LEFT, RIGHT = slice(0, N), slice(0, N // 2), slice(N // 2, N)
LOW, HIGH = slice(0, 2), slice(2, 4)
SHARE = 288


def chunk(c, n=1):
    return slice(c * P, (c + n) * P)


def tile_attend_x_mla_gate_seg_kernel(tc, qT, cT, ts, ch, og, offs, out):
    nc = tc.nc
    with ExitStack() as ctx:
        lists = ctx.enter_context(tc.tile_pool(name="lists", bufs=1))
        keep = ctx.enter_context(tc.tile_pool(name="keep", bufs=1))
        laid = ctx.enter_context(tc.tile_pool(name="laid", bufs=1))
        psum = ctx.enter_context(tc.psum_pool(name="psum", bufs=1))

        offsets = lists.tile([P, B * LIST], U16, name="offsets")

        def new(shape, dtype, name, tag=None):
            return keep.tile(shape, dtype, name=name, tag=tag or name, align_bytes=64)

        def lay(shape, dtype, name, offset):
            return laid.tile(shape, dtype, name=name, align_bytes=64, offset=offset)

        def each(shape, dtype, name):
            return [new(shape, dtype, f"{name}{b}") for b in range(B)]

        def new_bank(number, columns=N):
            return psum.tile([P, columns], F32, name="bank", tag=f"bank{number}")

        win = {(b, t): new([P, (b + 1) * SEG], F32, f"win{b}{t}") for b in range(B) for t in range(4 - b)}
        win[1, 3] = lay([P, T], F32, "win13", 6080)
        scale_tab = new([P, T], F32, "scale_tab")
        q_raw = each([P, 4, NQ], F32, "q_raw")
        ch_sb = new([P, D], F32, "ch_sb")
        og_sb = each([P, D], F32, "og_sb")
        planes = each([P, 4 * N], BF16, "planes")
        kb = each([P, 4 * N], BF16, "kb")
        k_codes, k_scales = each([P, N], U32, "k_codes"), each([P, N], U8, "k_scales")
        q_bf = each([P, NQ, 4], BF16, "q_bf")
        q_codes, q_scales = each([P, NQ], U32, "q_codes"), each([P, NQ], U8, "q_scales")
        tsg = each([P, N], F32, "tsg")
        ts_col = {0: new([P, 4], F32, "ts_col0")}
        ts_rows = {}
        neg_m, p, vb = {}, {}, {}
        a_t = each([P, 4, P], F32, "a_t")
        neg_m[1] = new([P, 1], F32, "neg_m1")
        p[1] = new([P, 4, P], F32, "p1")
        l_first = new([P, 1], F32, "l_first")
        l_part = new([P, 2], F32, "l_part")
        l_twice = new([P, B], F32, "l_twice")
        inv_l = new([P, B], F32, "inv_l")
        v_codes, v_scales = each([P, D], U32, "v_codes"), {}
        wb = each([P, NQ, 4], BF16, "wb")
        w_codes, w_scales = each([P, NQ], U32, "w_codes"), each([P, NQ], U8, "w_scales")
        th, o = each([P, D], F32, "th"), each([P, D], F32, "o")
        gate = {(0, 0): new([P, D], F32, "gate0"), (1, 0): new([P, D // 2], F32, "gate10")}
        bank = {}

        ident = new([P, P], F32, "ident")
        warm = new([P, 1], F32, "warm")
        warmed = new([P, 1], F32, "warmed")

        def preload_exp():
            nc.vector.memset(warm[:], 0.0)
            nc.scalar.activation(out=warmed[:], in_=warm[:], func=EXP)

        def build_identity():
            ones, ramp, turned = (new([P, 32], F32, name) for name in ("ones", "ramp", "turned"))
            nc.vector.memset(ones[:], 1.0)
            nc.vector.tensor_tensor_scan(ramp[:], ones[:], ones[:], -1.0, MULT, ADD)
            nc.vector.transpose(turned[:], ramp[:])
            nc.vector.memset(ident[:], 0.0)
            for first in range(0, P, 32):
                rows = slice(first, first + 32)
                nc.vector.tensor_tensor(ident[rows, rows], ramp[rows, :], turned[rows, :], EQUAL)

        def load_plane(b, t):
            cols = slice(b * SEG, (b + 1) * SEG)
            nc.sync.dma_start(out=win[b, t][:, cols], in_=cT.rearrange("(p t) n -> p t n", t=4)[:, t, cols])

        def load_scales():
            nc.scalar.dma_start(out=scale_tab[P - B : P, SEG:T], in_=ts[0].rearrange("(b n) -> b n", b=B))

        def clear_scales():
            nc.vector.memset(scale_tab[0 : P - B, SEG:T].bitcast(I32), 0)

        def load_queries(b):
            nc.sync.dma_start(out=q_raw[b][:], in_=qT[b].rearrange("(p t) q -> p t q", t=4))

        def load_channels():
            nc.sync.dma_start(out=ch_sb[:], in_=ch)

        def load_gate(b):
            nc.sync.dma_start(out=og_sb[b][:], in_=og[b])

        def move(engine, dst, src):
            if engine is nc.scalar:
                nc.scalar.activation(out=dst, in_=src, func=COPY)
            else:
                nc.vector.tensor_copy(out=dst, in_=src)

        def move_bits(engine, dst, src):
            if engine is nc.scalar:
                nc.scalar.copy(out=dst, in_=src)
            else:
                nc.vector.tensor_copy(out=dst, in_=src)

        def gather_plane(engine, b, t, cols=ALL):
            dst = planes[b][:, t * N + cols.start : t * N + cols.stop]
            move(engine, dst, win[b, t][:].indirect(offsets[:, b * LIST + cols.start // 16 : b * LIST + cols.stop // 16]))

        def gather_scales(engine, b):
            window = scale_tab[:] if b else scale_tab[:, SEG:T]
            move(engine, tsg[b][:], window.indirect(offsets[:, b * LIST : (b + 1) * LIST]))

        def weave(engine, b, cols):
            quads = slice(cols.start // 4, cols.stop // 4)
            dst = kb[b][:].rearrange("p (c i t) -> p c t i", i=4, t=4)[:, quads]
            src = planes[b][:].rearrange("p (t c i) -> p c t i", t=4, i=4)[:, quads]
            move_bits(engine, dst, src)

        def turn_scales(b, number):
            bank["ts", b] = new_bank(number)
            for j in range(4):
                nc.tensor.transpose(bank["ts", b][:, chunk(j)], tsg[b][:].rearrange("p (s j) -> p j s", j=4)[:, j, :], ident[:])

        def scale_columns(engine, b):
            move(engine, ts_col[b][:], bank["ts", b][:].rearrange("s (j r) -> s j r", j=4)[:, :, P - B + b])

        def spread_scales(b, number):
            bank["tsb", b] = new_bank(number)
            for j in range(4):
                nc.tensor.transpose(bank["tsb", b][:, chunk(j)], ts_col[b][:, j : j + 1].to_broadcast([P, P]), ident[:])

        def scale_rows(engine, b):
            move(engine, ts_rows[b][:].rearrange("q j s -> q (j s)"), bank["tsb", b][:])

        def cast_queries(engine, b):
            move(engine, q_bf[b][:].rearrange("p (c i) t -> p c t i", i=4), q_raw[b][:].rearrange("p t (c i) -> p c t i", i=4))

        def quantise(codes, scales, src):
            nc.vector.quantize_mx(out=codes.bitcast(FP8X4), scales=scales, in_=src)

        def quantise_queries(b):
            quantise(q_codes[b][:], q_scales[b][:], q_bf[b][:].rearrange("p n t -> p (n t)"))

        def quantise_keys(b, cols):
            quantise(k_codes[b][:, cols], k_scales[b][:, cols], kb[b][:, 4 * cols.start : 4 * cols.stop])

        def value_scales(b, cols):
            return v_scales[b][:, cols] if b else v_scales[b, cols.start // 256][:]

        def quantise_values(b, cols):
            quantise(v_codes[b][:, cols], value_scales(b, cols), vb[b][:] if b else vb[b, cols.start // 256][:])

        def quantise_weights(b, rows=slice(0, NQ)):
            quantise(w_codes[b][:, rows], w_scales[b][:, rows], wb[b][:, rows].rearrange("p n t -> p (n t)"))

        def multiply(dst, stationary, moving):
            nc.tensor.matmul_mx(
                out=dst,
                lhsT=stationary[0].bitcast(FP8X4),
                lhsT_scale=stationary[1],
                rhs=moving[0].bitcast(FP8X4),
                rhs_scale=moving[1],
                start=True,
                stop=True,
            )

        def scores(b, cols, place):
            multiply(place, (q_codes[b][:], q_scales[b][:]), (k_codes[b][:, cols], k_scales[b][:, cols]))

        def scale_scores(b, cols, place):
            rows = slice(cols.start // 4, cols.stop // 4)
            nc.vector.tensor_tensor(a_t[b][:, :, rows], place.rearrange("q (s j) -> q j s", j=4), ts_rows[b][:, :, rows], MULT)

        def maximum(b):
            nc.vector.tensor_reduce(out=neg_m[b][:], in_=a_t[b][:].rearrange("q j s -> q (j s)"), axis=AXIS_X, op=MAX, negate=True)

        def exponentials(b, js, total):
            nc.scalar.activation(out=p[b][:, js], in_=a_t[b][:, js], func=EXP, bias=neg_m[b][:], accum_out=total)

        def double_first_sum():
            nc.scalar.activation(out=l_twice[:, 0:1], in_=l_first[:], func=COPY, scale=2.0)

        def double_second_sum():
            nc.vector.tensor_scalar(l_twice[:, 1:2], l_part[:, 0:1], l_part[:, 1:2], 2.0, ADD, MULT)

        def invert_sums():
            nc.vector.reciprocal(inv_l[:], l_twice[:])

        def turn_values(b, t, place):
            words = planes[b][:, t * N : (t + 1) * N].bitcast(F32).rearrange("p (s h) -> p h s", h=2)
            for h in range(2):
                nc.tensor.transpose(place[:, chunk(h)], words[:, h, :], ident[:])

        def turn_first_values(t, number):
            bank["v", 0, t] = new_bank(number, 2 * P)
            turn_values(0, t, bank["v", 0, t])

        def copy_first_values(engine, t):
            dst = vb[0, t // 2][:].bitcast(F32)[:, chunk(2 * (t % 2), 2)].rearrange("s (p h) -> s p h", h=2)
            move_bits(engine, dst, bank["v", 0, t][:].rearrange("s (h p) -> s p h", h=2))

        def turn_last_values(number):
            bank["v", 0, 2] = new_bank(number)
            for t in range(2):
                turn_values(0, 2 + t, bank["v", 0, 2][:, chunk(2 * t, 2)])

        def copy_last_values():
            dst = vb[0, 1][:].bitcast(F32).rearrange("s (t p h) -> s t p h", t=2, h=2)
            nc.vector.tensor_copy(out=dst, in_=bank["v", 0, 2][:].rearrange("s (t h p) -> s t p h", t=2, h=2))

        def turn_second_values(u, number):
            bank["v", 1, u] = new_bank(number)
            for t in range(2):
                turn_values(1, 2 * u + t, bank["v", 1, u][:, chunk(2 * t, 2)])

        def copy_second_values(u):
            dst = vb[1][:].bitcast(F32).rearrange("s (p u w) -> s u p w", u=2, w=4)[:, u]
            nc.scalar.copy(out=dst, in_=bank["v", 1, u][:].rearrange("s (w p) -> s p w", w=4))

        def turn_weights(b, js, number=None):
            if js.start == 0:
                bank["w", b] = new_bank(number)
            for j in range(js.start, js.stop):
                nc.tensor.transpose(bank["w", b][:, chunk(j)], p[b][:, j, :], ident[:])

        def scale_weights(b, rows=slice(0, NQ)):
            pairs = slice(rows.start // 2, rows.stop // 2)
            nc.vector.tensor_tensor(
                wb[b][:].rearrange("s (q i) j -> s q j i", i=2)[:, pairs],
                bank["w", b][:].rearrange("s (j q i) -> s q j i", j=4, i=2)[:, pairs],
                ts_col[b][:].unsqueeze(1).unsqueeze(3).to_broadcast([P, pairs.stop - pairs.start, 4, 2]),
                MULT,
            )

        def products(b, cols, place):
            multiply(place, (w_codes[b][:], w_scales[b][:]), (v_codes[b][:, cols], value_scales(b, cols)))

        def gate_tanh(b):
            nc.scalar.activation(out=th[b][:], in_=og_sb[b][:], func=TANH, scale=0.5)

        def gate_channels(b, cols):
            nc.vector.scalar_tensor_tensor(out=gate[b, cols.start][:], in0=th[b][:, cols], scalar=1.0, in1=ch_sb[:, cols], op0=ADD, op1=MULT)

        def finish(b, cols, y):
            dst, factor = o[b][:, cols], gate[b, cols.start][:] if b else gate[b, 0][:, cols]
            if b == 0:
                y = y.rearrange("q (t p) -> q p t", t=4)[:, cols.start // 4 : cols.stop // 4]
                dst, factor = dst.rearrange("q (p t) -> q p t", t=4), factor.rearrange("q (p t) -> q p t", t=4)
            nc.vector.scalar_tensor_tensor(out=dst, in0=y, scalar=inv_l[:, b : b + 1], in1=factor, op0=MULT, op1=MULT)
            nc.sync.dma_start(out=out[b][:, cols], in_=o[b][:, cols])

        nc.sync.dma_start(offsets[:], offs)
        load_scales()
        for t in range(4):
            load_plane(0, t)
        load_queries(0)
        for t in range(4):
            load_plane(1, t)
        load_queries(1)
        load_gate(0)
        load_gate(1)
        load_channels()
        preload_exp()
        build_identity()
        clear_scales()
        gather_scales(nc.vector, 0)
        gather_scales(nc.scalar, 1)
        gather_plane(nc.scalar, 0, 0)
        turn_scales(0, 0)
        scale_columns(nc.scalar, 0)
        gather_plane(nc.vector, 0, 1)
        turn_first_values(0, 0)
        spread_scales(0, 1)
        gather_plane(nc.scalar, 0, 2)
        turn_first_values(1, 3)
        early = new([P, D + N], F32, "early", tag="win01")
        vb[0, 0] = early[:, 0:D].bitcast(BF16)
        ts_rows[0] = early[:, D : D + N].rearrange("q (j s) -> q j s", j=4)
        copy_first_values(nc.vector, 0)
        scale_rows(nc.vector, 0)
        copy_first_values(nc.vector, 1)
        gather_plane(nc.scalar, 0, 3, LEFT)
        gather_plane(nc.scalar, 0, 3, RIGHT)
        turn_last_values(4)
        turn_scales(1, 1)
        cast_queries(nc.vector, 0)
        weave(nc.vector, 0, LEFT)
        weave(nc.vector, 0, RIGHT)
        vb[0, 1] = new([P, 2 * D], BF16, "vb01", tag="win03")
        quantise_keys(0, LEFT)
        quantise_queries(0)
        quantise_keys(0, RIGHT)
        gather_plane(nc.scalar, 1, 0)
        first_scores = new_bank(0)
        scores(0, LEFT, first_scores[:, LEFT])
        scores(0, RIGHT, first_scores[:, RIGHT])
        v_scales[0, 0] = new([P, D // 2], U8, "v_scales00", tag="q_raw0")
        quantise_values(0, LEFT)
        copy_last_values()
        ts_col[1] = new([P, 4], F32, "ts_col1", tag="kb0")
        scale_columns(nc.vector, 1)
        spread_scales(1, 6)
        gather_plane(nc.scalar, 1, 1, slice(0, SHARE))
        gather_plane(nc.vector, 1, 1, slice(SHARE, N))
        scale_scores(0, ALL, first_scores[:])
        gather_plane(nc.scalar, 1, 2)
        v_scales[0, 1] = new([P, D // 2], U8, "v_scales01", tag="win11")
        quantise_values(0, RIGHT)
        neg_m[0] = new([P, 1], F32, "neg_m0")
        maximum(0)
        turn_second_values(0, 0)
        for c in range(4):
            gather_plane(nc.scalar, 1, 3, chunk(c))
        weave(nc.vector, 1, chunk(0))
        weave(nc.vector, 1, chunk(1))
        cast_queries(nc.vector, 1)
        weave(nc.vector, 1, chunk(2))
        weave(nc.vector, 1, chunk(3))
        late = lay([P, N + 2 * D], F32, "late", 0)
        p[0] = late[:, 0:N].rearrange("q (j s) -> q j s", j=4)
        vb[1] = late[:, N : N + 2 * D].bitcast(BF16)
        ts_rows[1] = lay([P, 4, P], F32, "ts_rows1", 14208)
        quantise_queries(1)
        quantise_keys(1, LEFT)
        quantise_keys(1, RIGHT)
        turn_second_values(1, 1)
        left_scores, right_scores = new_bank(2, N // 2), new_bank(3, N // 2)
        scores(1, LEFT, left_scores[:])
        scores(1, RIGHT, right_scores[:])
        gate_tanh(0)
        scale_rows(nc.scalar, 1)
        gate_tanh(1)
        exponentials(0, slice(0, 4), l_first[:])
        copy_second_values(0)
        copy_second_values(1)
        double_first_sum()
        gate_channels(0, ALL)
        scale_scores(1, LEFT, left_scores[:])
        scale_scores(1, RIGHT, right_scores[:])
        turn_weights(0, slice(0, 4), 3)
        gate_channels(1, LEFT)
        maximum(1)
        v_scales[1] = lay([P, D], U8, "v_scales1", 14272)
        gate[1, RIGHT.start] = lay([P, D // 2], F32, "gate11", 14784)
        gate_channels(1, RIGHT)
        scale_weights(0)
        quantise_values(1, ALL)
        quantise_weights(0)
        for js in (LOW, HIGH):
            exponentials(1, js, l_part[:, js.start // 2 : js.stop // 2])
            turn_weights(1, js, 6)
        first_products = new_bank(7)
        products(0, LEFT, first_products[:, LEFT])
        products(0, RIGHT, first_products[:, RIGHT])
        double_second_sum()
        scale_weights(1, slice(0, 64))
        scale_weights(1, slice(64, NQ))
        quantise_weights(1, slice(0, 64))
        invert_sums()
        quantise_weights(1, slice(64, NQ))
        left_products, right_products = new_bank(0, N // 2), new_bank(4, N // 2)
        products(1, LEFT, left_products[:])
        products(1, RIGHT, right_products[:])
        finish(0, LEFT, first_products[:])
        finish(0, RIGHT, first_products[:])
        finish(1, LEFT, left_products[:])
        finish(1, RIGHT, right_products[:])
